import numpy as np
import ml_dtypes


def mxq(x, axis, fmt="e4m3"):
    dtype, down = {"e4m3": (ml_dtypes.float8_e4m3fn, 7), "e5m2": (ml_dtypes.float8_e5m2, 14)}[fmt]
    v = np.moveaxis(np.asarray(x, np.float32).astype(ml_dtypes.bfloat16).astype(np.float64), axis, -1)
    blocks = v.reshape(v.shape[:-1] + (-1, 32))
    amax = np.abs(blocks).max(-1, keepdims=True)
    byte = np.maximum(np.where(amax > 0, np.frexp(amax)[1] - 1 + 127, 0) - down, 1)
    scale = np.exp2(byte - 127.0)
    codes = (blocks / scale).astype(np.float32).astype(dtype).astype(np.float64)
    return np.moveaxis((codes * scale).reshape(v.shape), -1, axis)


WIDE = False


def mx_kscale(k):
    if not WIDE:
        return np.ones(k)
    levels = np.array([10, -10, 5, -5, 0])
    if k % 512:
        return np.exp2(np.random.permutation(np.resize(levels, k // 32))).repeat(32)
    a = np.empty((k // 512, 16))
    for p in range(k // 512):
        a[p, :8] = np.random.permutation(np.resize(levels, 8))
        for g in range(8):
            far = levels[np.abs(levels - a[p, g]) >= 10]
            a[p, g + 8] = far[np.random.randint(len(far))]
    return np.exp2(a.ravel()).repeat(32)


def f64(x):
    return np.asarray(x).astype(np.float64)


def striped(idx):
    return np.tile(idx.reshape(-1, 16).T, (8, 1)).astype(np.uint16)


def unstriped(offs):
    return offs[:16].T.reshape(-1).astype(np.int64)


E2M1 = np.array([0.0, 0.5, 1.0, 1.5, 2.0, 3.0, 4.0, 6.0, -0.0, -0.5, -1.0, -1.5, -2.0, -3.0, -4.0, -6.0])


def pack_weight(w, fmt):
    k, n = w.shape
    w = f64(np.asarray(w, np.float32).astype(ml_dtypes.bfloat16)).reshape(k // 32, 32, n)
    amax = np.abs(w).max(1)
    if fmt == "e4m3":
        byte = np.frexp(amax)[1] - 1 + 127 - 7
    else:
        mant, ex = np.frexp(amax / 6.0)
        byte = np.where(mant > 0.5, ex, ex - 1) + 127
    byte = np.clip(np.where(amax > 0, byte, 1), 1, 254)
    scaled = (w * np.exp2(127.0 - byte)[:, None, :]).reshape(k, n).astype(np.float32)
    by_word = np.ascontiguousarray(scaled.reshape(k // 512, 128, 4, n).transpose(0, 1, 3, 2))
    if fmt == "e4m3":
        words = by_word.astype(ml_dtypes.float8_e4m3fn).view(np.uint8)
    else:
        c = by_word.astype(ml_dtypes.float4_e2m1fn).view(np.uint8) & 0xF
        words = (c[..., 0::2] | (c[..., 1::2] << 4)).reshape(k // 512, 128, 2 * n)
    return np.ascontiguousarray(words), np.ascontiguousarray(byte.astype(np.uint8).reshape(k // 512, 16, n))


def unpack_weight(words, scales, fmt):
    g, _, n = scales.shape
    words = np.ascontiguousarray(words).reshape(g, 128, n, -1)
    if fmt == "e4m3":
        vals = words.view(ml_dtypes.float8_e4m3fn).astype(np.float64)
    else:
        nib = np.empty((g, 128, n, 4), np.uint8)
        nib[..., 0::2] = words & 0xF
        nib[..., 1::2] = words >> 4
        vals = E2M1[nib]
    vals = vals * np.repeat(np.exp2(scales.astype(np.float64) - 127.0), 8, axis=1)[..., None]
    return vals.transpose(0, 1, 3, 2).reshape(g * 512, n)


K, T, E, C, H, N = 128, 512, 2, 256, 512, 512


def by_expert(wq, xq):
    return np.concatenate([wq[e].T @ xq[:, e * C:(e + 1) * C] for e in range(E)], axis=1)


def setup_inputs():
    n = np.random.standard_normal
    v = mx_kscale(N)
    u = mx_kscale(H)
    slot_token = np.random.permutation(T)[:E * C]
    w_slot = np.random.uniform(0.2, 1.0, E * C)
    dy = pack_weight(n((N, T)) * v[:, None], "e4m3")
    wt = pack_weight(n((N, K)) / np.sqrt(N) / v[:, None], "e2m1")
    wbt = [pack_weight(m, "e2m1") for m in n((E, N, H)) / np.sqrt(N) / v[None, :, None] * u]
    wat = [pack_weight(m, "e2m1") for m in n((E, H, K)) / np.sqrt(H) / u[None, :, None]]
    return {
        "dy_words": dy[0],
        "dy_scales": dy[1],
        "wt_words": wt[0],
        "wt_scales": wt[1],
        "wbt_words": np.stack([m[0] for m in wbt]),
        "wbt_scales": np.stack([m[1] for m in wbt]),
        "wat_words": np.stack([m[0] for m in wat]),
        "wat_scales": np.stack([m[1] for m in wat]),
        "gate": (np.tile(w_slot, (128, 1))).astype(np.float32),
        "offs": striped(slot_token),
    }


def reference(dy_words, dy_scales, wt_words, wt_scales, wbt_words, wbt_scales, wat_words, wat_scales, gate, offs):
    wt = unpack_weight(wt_words, wt_scales, "e2m1")
    wbt = np.stack([unpack_weight(wbt_words[e], wbt_scales[e], "e2m1") for e in range(E)])
    wat = np.stack([unpack_weight(wat_words[e], wat_scales[e], "e2m1") for e in range(E)])
    idx = unstriped(offs)
    dy = unpack_weight(dy_words, dy_scales, "e4m3")
    base = wt.T @ dy
    dh = f64(gate[:1]) * by_expert(wbt, dy[:, idx])
    dx = by_expert(wat, mxq(dh, 0, "e4m3"))
    c = np.zeros((K, T))
    c[:, idx] = dx
    return base + c

@@ -1,0 +1,183 @@
+from contextlib import ExitStack
+
+import concourse.mybir as mybir
+from concourse.masks import make_identity
+
+K, T, E, C, H, N = 128, 512, 2, 256, 512, 512
+FLOPS = 2 * (N * K * T + N * H * T + H * K * T)
+
+F32 = mybir.dt.float32
+BF16 = mybir.dt.bfloat16
+I32 = mybir.dt.int32
+U32 = mybir.dt.uint32
+U16 = mybir.dt.uint16
+U8 = mybir.dt.uint8
+FP8X4 = mybir.dt.float8_e4m3fn_x4
+FP4X4 = mybir.dt.float4_e2m1fn_x4
+COPY = mybir.ActivationFunctionType.Copy
+ADD = mybir.AluOpType.add
+MULT = mybir.AluOpType.mult
+
+P = 128
+BLK = 128
+NB = T // BLK
+
+
+def load_plane_filled(queue, plane, rows):
+    words = rows.bitcast(I32)
+    width = words.shape[1]
+    for q in range(4):
+        src = words[4 * q : 4 * q + 4, :].unsqueeze(0).broadcast_to([8, 4, width])
+        queue.dma_start(out=plane[32 * q : 32 * q + 32, :].bitcast(I32), in_=src)
+
+
+def load_planes(queue, planes, rows):
+    words = rows.bitcast(I32).rearrange("e b c -> b e c")
+    for q in range(4):
+        queue.dma_start(out=planes[32 * q : 32 * q + 4, :, :].bitcast(I32), in_=words[4 * q : 4 * q + 4, :, :])
+
+
+def tile_moe_adb_none_kernel(
+    tc, dy_words, dy_scales, wt_words, wt_scales, wbt_words, wbt_scales, wat_words, wat_scales, gate, offs, out
+):
+    nc = tc.nc
+    with ExitStack() as ctx:
+        keep = ctx.enter_context(tc.tile_pool(name="keep", bufs=1))
+        psum = ctx.enter_context(tc.psum_pool(name="psum", bufs=1))
+
+        offsets = keep.tile([P, T // 16], U16, name="offsets")
+        dyw = keep.tile([P, T], U32, name="dyw", align_bytes=64)
+        dys = keep.tile([P, T], U8, name="dys", align_bytes=64)
+        wbw = keep.tile([P, E, 2 * H], U8, name="wbw", align_bytes=64)
+        wbs = keep.tile([P, E, H], U8, name="wbs", align_bytes=64)
+        waw = keep.tile([P, E, 2 * K], U8, name="waw", align_bytes=64)
+        was = keep.tile([P, E, K], U8, name="was", align_bytes=64)
+        wtw = keep.tile([P, 2 * K], U8, name="wtw", align_bytes=64)
+        wts = keep.tile([P, 1, K], U8, name="wts", align_bytes=64)
+        g = keep.tile([P, NB], F32, name="g")
+        ident = keep.tile([P, P], F32, name="ident")
+        warm_in = keep.tile([P, 1], F32, name="warm_in")
+        warm_out = keep.tile([P, 1], BF16, name="warm_out")
+
+        for planes in (wbs, was, wts):
+            nc.vector.memset(planes[:].bitcast(I32), 0)
+        nc.vector.memset(warm_in[:], 0.0)
+        nc.scalar.activation(out=warm_out[:], in_=warm_in[:], func=COPY)
+        make_identity(nc, ident[:])
+
+        nc.sync.dma_start(offsets[:], offs)
+        load_plane_filled(nc.sync, dys, dy_scales[0])
+        nc.sync.dma_start(out=dyw[:].bitcast(I32), in_=dy_words[0].rearrange("p t d -> p (t d)").bitcast(I32))
+        nc.sync.dma_start(
+            out=wbw[:].bitcast(I32), in_=wbt_words[:, 0].rearrange("e p c -> p e c").bitcast(I32)
+        )
+        load_planes(nc.sync, wbs, wbt_scales[:, 0])
+        with nc.allow_non_contiguous_dma(reason="one weight a slot, a slot a partition"):
+            nc.sync.dma_start(out=g[:], in_=gate[0].rearrange("(b p) -> p b", p=P))
+        nc.sync.dma_start(
+            out=waw[:].bitcast(I32), in_=wat_words[:, 0].rearrange("e p c -> p e c").bitcast(I32)
+        )
+        load_planes(nc.sync, was, wat_scales[:, 0])
+        nc.sync.dma_start(out=wtw[:].bitcast(I32), in_=wt_words[0].bitcast(I32))
+        load_planes(nc.sync, wts, wt_scales)
+
+        gw = [keep.tile([P, BLK], U32, name="gw%d" % b, align_bytes=64) for b in range(NB)]
+        gs = [keep.tile([P, C], U8, name="gs%d" % e, align_bytes=64) for e in range(E)]
+        hb = {}
+        dx = {}
+        dq = [keep.tile([P, 4 * BLK], BF16, name="dq%d" % b, align_bytes=64) for b in range(NB)]
+        hw = [keep.tile([P, BLK], U32, name="hw%d" % b, align_bytes=64) for b in range(NB)]
+        hs = [keep.tile([P, BLK], U8, name="hs%d" % b, align_bytes=64) for b in range(NB)]
+        window = keep.tile([P, T], F32, name="window", align_bytes=64)
+        res = [keep.tile([P, T // 2], F32, name="res%d" % h, align_bytes=64) for h in range(2)]
+
+        def offs_of(b):
+            return offsets[:, b * (BLK // 16) : (b + 1) * (BLK // 16)]
+
+        def gather(b):
+            nc.vector.tensor_copy(gw[b][:], dyw[:].indirect(offs_of(b)))
+
+        def product(b, bank, i0, width):
+            e = b * BLK // C
+            acc = psum.tile([P, width], F32, name="acc_h", tag=bank)
+            nc.tensor.matmul_mx(
+                out=acc[:], lhsT=gw[b][:].bitcast(FP8X4), lhsT_scale=gs[e][:, b * BLK % C : b * BLK % C + BLK],
+                rhs=wbw[:, e, 2 * i0 : 2 * (i0 + width)].bitcast(FP4X4), rhs_scale=wbs[:, e, i0 : i0 + width],
+                start=True, stop=True,
+            )
+            dst = hb[b][:].rearrange("s (u p d) -> s u p d", u=2, d=2)[:, :, i0 // 4 : (i0 + width) // 4, :]
+            return dst, acc[:].rearrange("s (p u d) -> s u p d", u=2, d=2)
+
+        def first(b, *banks):
+            hb[b] = keep.tile([P, H], BF16, name="hb%d" % b, tag="hb%d" % b, align_bytes=64)
+            width = H // len(banks)
+            dst, src = product(b, banks[0], 0, width)
+            nc.scalar.activation(out=dst, in_=src, func=COPY, scale=g[:, b : b + 1])
+            if len(banks) == 2:
+                dst, src = product(b, banks[1], width, width)
+                nc.vector.tensor_scalar(out=dst, in0=src, scalar1=g[:, b : b + 1], scalar2=None, op0=MULT)
+
+        def turn(b, bank):
+            pairs = hb[b][:].bitcast(F32)
+            turned = psum.tile([P, 2, BLK], F32, name="turned", tag=bank)
+            for u in range(2):
+                nc.tensor.transpose(turned[:, u, :], pairs[:, u * P : (u + 1) * P], ident[:])
+            dst = dq[b][:].bitcast(F32).rearrange("p (s u) -> p s u", u=2)
+            src = turned[:].rearrange("p u s -> p s u")
+            if b < 2:
+                nc.vector.tensor_copy(out=dst, in_=src)
+            else:
+                nc.scalar.copy(out=dst, in_=src)
+
+        def quantise(b):
+            nc.vector.quantize_mx(out=hw[b][:].bitcast(FP8X4), scales=hs[b][:], in_=dq[b][:])
+
+        def second(b, bank, tag):
+            e = b * BLK // C
+            acc = psum.tile([P, BLK], F32, name="acc_x", tag=bank)
+            nc.tensor.matmul_mx(
+                out=acc[:], lhsT=waw[:, e, :].bitcast(FP4X4), lhsT_scale=was[:, e, :],
+                rhs=hw[b][:].bitcast(FP8X4), rhs_scale=hs[b][:], start=True, stop=True,
+            )
+            dx[b] = keep.tile([P, BLK], F32, name="dx%d" % b, tag=tag, align_bytes=64)
+            if b == 0:
+                nc.vector.tensor_copy(out=dx[b][:], in_=acc[:])
+            else:
+                nc.scalar.copy(out=dx[b][:], in_=acc[:])
+
+        def scatter(b):
+            nc.vector.tensor_copy(window[:].indirect(offs_of(b)), dx[b][:])
+
+        for e in range(E):
+            nc.vector.tensor_copy(gs[e][:], dys[:].indirect(offsets[:, e * (C // 16) : (e + 1) * (C // 16)]))
+            gather(2 * e)
+            gather(2 * e + 1)
+        first(0, "A", "B")
+        first(1, "C")
+        turn(0, "D")
+        first(2, "B")
+        quantise(0)
+        turn(1, "E")
+        first(3, "D")
+        second(0, "F", "dx0")
+        quantise(1)
+        turn(2, "A")
+        scatter(0)
+        second(1, "G", "hb2")
+        quantise(2)
+        turn(3, "B")
+        scatter(1)
+        second(2, "H", "hb3")
+        quantise(3)
+        second(3, "C", "dx3")
+        base = psum.tile([P, T], F32, name="base", tag="A")
+        nc.tensor.matmul_mx(
+            out=base[:], lhsT=wtw[:].bitcast(FP4X4), lhsT_scale=wts[:, 0, :],
+            rhs=dyw[:].bitcast(FP8X4), rhs_scale=dys[:], start=True, stop=True,
+        )
+        scatter(2)
+        scatter(3)
+        for h, queue in enumerate((nc.sync, nc.scalar)):
+            cols = slice(h * (T // 2), (h + 1) * (T // 2))
+            nc.vector.tensor_tensor(out=res[h][:], in0=base[:, cols], in1=window[:, cols], op=ADD)
+            queue.dma_start(out=out[:, cols], in_=res[h][:])

@@ -50,14 +50,12 @@ def tile_moe_adb_none_kernel(
         dys = keep.tile([P, T], U8, name="dys", align_bytes=64)
         wbw = keep.tile([P, E, 2 * H], U8, name="wbw", align_bytes=64)
         wbs = keep.tile([P, E, H], U8, name="wbs", align_bytes=64)
-        waw = keep.tile([P, E, 2 * K], U8, name="waw", align_bytes=64)
         was = keep.tile([P, E, K], U8, name="was", align_bytes=64)
-        wtw = keep.tile([P, 2 * K], U8, name="wtw", align_bytes=64)
         wts = keep.tile([P, 1, K], U8, name="wts", align_bytes=64)
         g = keep.tile([P, NB], F32, name="g")
         ident = keep.tile([P, P], F32, name="ident")
-        warm_in = keep.tile([P, 1], F32, name="warm_in")
-        warm_out = keep.tile([P, 1], BF16, name="warm_out")
+        warm_in = keep.tile([P, 1], F32, name="warm_in", tag="warm_in", align_bytes=64)
+        warm_out = keep.tile([P, 1], BF16, name="warm_out", tag="warm_out", align_bytes=64)
 
         for planes in (wbs, was, wts):
             nc.vector.memset(planes[:].bitcast(I32), 0)
@@ -74,19 +72,21 @@ def tile_moe_adb_none_kernel(
         load_planes(nc.sync, wbs, wbt_scales[:, 0])
         with nc.allow_non_contiguous_dma(reason="one weight a slot, a slot a partition"):
             nc.sync.dma_start(out=g[:], in_=gate[0].rearrange("(b p) -> p b", p=P))
+        load_planes(nc.sync, was, wat_scales[:, 0])
+        waw = keep.tile([P, E, 2 * K], U8, name="waw", tag="warm_out", align_bytes=64)
         nc.sync.dma_start(
             out=waw[:].bitcast(I32), in_=wat_words[:, 0].rearrange("e p c -> p e c").bitcast(I32)
         )
-        load_planes(nc.sync, was, wat_scales[:, 0])
+        wtw = keep.tile([P, 2 * K], U8, name="wtw", tag="warm_in", align_bytes=64)
         nc.sync.dma_start(out=wtw[:].bitcast(I32), in_=wt_words[0].bitcast(I32))
         load_planes(nc.sync, wts, wt_scales)
 
-        gw = [keep.tile([P, BLK], U32, name="gw%d" % b, align_bytes=64) for b in range(NB)]
+        gw = {}
         gs = [keep.tile([P, C], U8, name="gs%d" % e, align_bytes=64) for e in range(E)]
         hb = {}
         dx = {}
-        dq = [keep.tile([P, 4 * BLK], BF16, name="dq%d" % b, align_bytes=64) for b in range(NB)]
-        hw = [keep.tile([P, BLK], U32, name="hw%d" % b, align_bytes=64) for b in range(NB)]
+        dq = {}
+        hw = [keep.tile([P, BLK], U32, name="hw%d" % b, tag="hw%d" % b, align_bytes=64) for b in range(NB)]
         hs = [keep.tile([P, BLK], U8, name="hs%d" % b, align_bytes=64) for b in range(NB)]
         window = keep.tile([P, T], F32, name="window", align_bytes=64)
         res = [keep.tile([P, T // 2], F32, name="res%d" % h, align_bytes=64) for h in range(2)]
@@ -94,7 +94,8 @@ def tile_moe_adb_none_kernel(
         def offs_of(b):
             return offsets[:, b * (BLK // 16) : (b + 1) * (BLK // 16)]
 
-        def gather(b):
+        def gather(b, tag):
+            gw[b] = keep.tile([P, BLK], U32, name="gw%d" % b, tag=tag, align_bytes=64)
             nc.vector.tensor_copy(gw[b][:], dyw[:].indirect(offs_of(b)))
 
         def product(b, bank, i0, width):
@@ -108,20 +109,22 @@ def tile_moe_adb_none_kernel(
             dst = hb[b][:].rearrange("s (u p d) -> s u p d", u=2, d=2)[:, :, i0 // 4 : (i0 + width) // 4, :]
             return dst, acc[:].rearrange("s (p u d) -> s u p d", u=2, d=2)
 
-        def first(b, *banks):
-            hb[b] = keep.tile([P, H], BF16, name="hb%d" % b, tag="hb%d" % b, align_bytes=64)
+        def first(b, tag, *banks):
+            hb[b] = keep.tile([P, H], BF16, name="hb%d" % b, tag=tag, align_bytes=64)
             width = H // len(banks)
+            weight = g[:, b : b + 1]
             dst, src = product(b, banks[0], 0, width)
-            nc.scalar.activation(out=dst, in_=src, func=COPY, scale=g[:, b : b + 1])
+            nc.scalar.activation(out=dst, in_=src, func=COPY, scale=weight)
             if len(banks) == 2:
                 dst, src = product(b, banks[1], width, width)
-                nc.vector.tensor_scalar(out=dst, in0=src, scalar1=g[:, b : b + 1], scalar2=None, op0=MULT)
+                nc.vector.tensor_scalar(out=dst, in0=src, scalar1=weight, scalar2=None, op0=MULT)
 
         def turn(b, bank):
             pairs = hb[b][:].bitcast(F32)
             turned = psum.tile([P, 2, BLK], F32, name="turned", tag=bank)
             for u in range(2):
                 nc.tensor.transpose(turned[:, u, :], pairs[:, u * P : (u + 1) * P], ident[:])
+            dq[b] = keep.tile([P, 4 * BLK], BF16, name="dq%d" % b, tag="dq%d" % max(b, 1), align_bytes=64)
             dst = dq[b][:].bitcast(F32).rearrange("p (s u) -> p s u", u=2)
             src = turned[:].rearrange("p u s -> p s u")
             if b < 2:
@@ -148,29 +151,34 @@ def tile_moe_adb_none_kernel(
         def scatter(b):
             nc.vector.tensor_copy(window[:].indirect(offs_of(b)), dx[b][:])
 
-        for e in range(E):
+        def gather_scales(e):
             nc.vector.tensor_copy(gs[e][:], dys[:].indirect(offsets[:, e * (C // 16) : (e + 1) * (C // 16)]))
-            gather(2 * e)
-            gather(2 * e + 1)
-        first(0, "A", "B")
-        first(1, "C")
-        turn(0, "D")
-        first(2, "B")
+
+        gather_scales(0)
+        gather(0, "gw0")
+        gather(1, "gw1")
+        gather_scales(1)
+        gather(2, "gw2")
+        first(0, "hb0", "A", "B")
+        first(1, "hb1", "C")
+        first(2, "hb2", "D")
+        turn(0, "E")
+        gather(3, "hb0")
         quantise(0)
-        turn(1, "E")
-        first(3, "D")
-        second(0, "F", "dx0")
+        turn(1, "F")
+        second(0, "G", "dx0")
         quantise(1)
-        turn(2, "A")
+        first(3, "hw0", "E")
+        turn(2, "G")
         scatter(0)
-        second(1, "G", "hb2")
         quantise(2)
-        turn(3, "B")
+        turn(3, "H")
+        second(1, "B", "hw0")
         scatter(1)
-        second(2, "H", "hb3")
         quantise(3)
+        second(2, "H", "dx2")
         second(3, "C", "dx3")
-        base = psum.tile([P, T], F32, name="base", tag="A")
+        base = psum.tile([P, T], F32, name="base", tag="B")
         nc.tensor.matmul_mx(
             out=base[:], lhsT=wtw[:].bitcast(FP4X4), lhsT_scale=wts[:, 0, :],
             rhs=dyw[:].bitcast(FP8X4), rhs_scale=dys[:], start=True, stop=True,

@@ -19,21 +19,24 @@ ADD = mybir.AluOpType.add
 MULT = mybir.AluOpType.mult
 
 P = 128
-BLK = 128
-NB = T // BLK
+GROUP = 128
+GROUPS = T // GROUP
+PER_COLUMN = 16
+QUADRANTS = 4
+FIRST_STORE = 384
 
 
 def load_plane_filled(queue, plane, rows):
     words = rows.bitcast(I32)
     width = words.shape[1]
-    for q in range(4):
-        src = words[4 * q : 4 * q + 4, :].unsqueeze(0).broadcast_to([8, 4, width])
-        queue.dma_start(out=plane[32 * q : 32 * q + 32, :].bitcast(I32), in_=src)
+    for q in range(QUADRANTS):
+        repeated = words[4 * q : 4 * q + 4, :].unsqueeze(0).broadcast_to([8, 4, width])
+        queue.dma_start(out=plane[32 * q : 32 * q + 32, :].bitcast(I32), in_=repeated)
 
 
 def load_planes(queue, planes, rows):
-    words = rows.bitcast(I32).rearrange("e b c -> b e c")
-    for q in range(4):
+    words = rows.bitcast(I32).rearrange("e c x -> c e x")
+    for q in range(QUADRANTS):
         queue.dma_start(out=planes[32 * q : 32 * q + 4, :, :].bitcast(I32), in_=words[4 * q : 4 * q + 4, :, :])
 
 
@@ -45,147 +48,150 @@ def tile_moe_adb_none_kernel(
         keep = ctx.enter_context(tc.tile_pool(name="keep", bufs=1))
         psum = ctx.enter_context(tc.psum_pool(name="psum", bufs=1))
 
-        offsets = keep.tile([P, T // 16], U16, name="offsets")
-        dyw = keep.tile([P, T], U32, name="dyw", align_bytes=64)
-        dys = keep.tile([P, T], U8, name="dys", align_bytes=64)
-        wbw = keep.tile([P, E, 2 * H], U8, name="wbw", align_bytes=64)
-        wbs = keep.tile([P, E, H], U8, name="wbs", align_bytes=64)
-        was = keep.tile([P, E, K], U8, name="was", align_bytes=64)
-        wts = keep.tile([P, 1, K], U8, name="wts", align_bytes=64)
-        g = keep.tile([P, NB], F32, name="g")
-        ident = keep.tile([P, P], F32, name="ident")
+        offsets = keep.tile([P, T // PER_COLUMN], U16, name="offsets")
+        dy_w = keep.tile([P, T], U32, name="dy_w", align_bytes=64)
+        dy_s = keep.tile([P, T], U8, name="dy_s", align_bytes=64)
+        wb_w = keep.tile([P, E, 2 * H], U8, name="wb_w", align_bytes=64)
+        wb_s = keep.tile([P, E, H], U8, name="wb_s", align_bytes=64)
+        wa_s = keep.tile([P, E, K], U8, name="wa_s", align_bytes=64)
+        wt_s = keep.tile([P, 1, K], U8, name="wt_s", align_bytes=64)
+        gates = keep.tile([P, GROUPS], F32, name="gates")
+        identity = keep.tile([P, P], F32, name="identity")
         warm_in = keep.tile([P, 1], F32, name="warm_in", tag="warm_in", align_bytes=64)
         warm_out = keep.tile([P, 1], BF16, name="warm_out", tag="warm_out", align_bytes=64)
 
-        for planes in (wbs, was, wts):
+        for planes in (wb_s, wa_s, wt_s):
             nc.vector.memset(planes[:].bitcast(I32), 0)
         nc.vector.memset(warm_in[:], 0.0)
         nc.scalar.activation(out=warm_out[:], in_=warm_in[:], func=COPY)
-        make_identity(nc, ident[:])
+        make_identity(nc, identity[:])
 
         nc.sync.dma_start(offsets[:], offs)
-        load_plane_filled(nc.sync, dys, dy_scales[0])
-        nc.sync.dma_start(out=dyw[:].bitcast(I32), in_=dy_words[0].rearrange("p t d -> p (t d)").bitcast(I32))
+        load_plane_filled(nc.sync, dy_s, dy_scales[0])
+        nc.sync.dma_start(out=dy_w[:].bitcast(I32), in_=dy_words[0].rearrange("p t d -> p (t d)").bitcast(I32))
+        wt_w = keep.tile([P, 2 * K], U8, name="wt_w", align_bytes=64)
+        nc.sync.dma_start(out=wt_w[:].bitcast(I32), in_=wt_words[0].bitcast(I32))
         nc.sync.dma_start(
-            out=wbw[:].bitcast(I32), in_=wbt_words[:, 0].rearrange("e p c -> p e c").bitcast(I32)
+            out=wb_w[:].bitcast(I32), in_=wbt_words[:, 0].rearrange("e p x -> p e x").bitcast(I32)
         )
-        load_planes(nc.sync, wbs, wbt_scales[:, 0])
+        load_planes(nc.sync, wb_s, wbt_scales[:, 0])
         with nc.allow_non_contiguous_dma(reason="one weight a slot, a slot a partition"):
-            nc.sync.dma_start(out=g[:], in_=gate[0].rearrange("(b p) -> p b", p=P))
-        load_planes(nc.sync, was, wat_scales[:, 0])
-        waw = keep.tile([P, E, 2 * K], U8, name="waw", tag="warm_out", align_bytes=64)
+            nc.sync.dma_start(out=gates[:], in_=gate[0].rearrange("(b s) -> s b", s=GROUP))
+        load_planes(nc.sync, wa_s, wat_scales[:, 0])
+        wa_w = keep.tile([P, E, 2 * K], U8, name="wa_w", tag="warm_out", align_bytes=64)
         nc.sync.dma_start(
-            out=waw[:].bitcast(I32), in_=wat_words[:, 0].rearrange("e p c -> p e c").bitcast(I32)
+            out=wa_w[:].bitcast(I32), in_=wat_words[:, 0].rearrange("e p x -> p e x").bitcast(I32)
         )
-        wtw = keep.tile([P, 2 * K], U8, name="wtw", tag="warm_in", align_bytes=64)
-        nc.sync.dma_start(out=wtw[:].bitcast(I32), in_=wt_words[0].bitcast(I32))
-        load_planes(nc.sync, wts, wt_scales)
+        warm_sums = psum.tile([P, T], F32, name="warm_sums", tag="H")
+        for width in (T, T // 2):
+            nc.tensor.matmul_mx(
+                out=warm_sums[:, :width], lhsT=wt_w[:].bitcast(FP4X4), lhsT_scale=wt_s[:, 0, :],
+                rhs=dy_w[:, :width].bitcast(FP8X4), rhs_scale=dy_s[:, :width], start=True, stop=True,
+            )
+        load_planes(nc.sync, wt_s, wt_scales)
 
-        gw = {}
-        gs = [keep.tile([P, C], U8, name="gs%d" % e, align_bytes=64) for e in range(E)]
-        hb = {}
-        dx = {}
-        dq = {}
-        hw = [keep.tile([P, BLK], U32, name="hw%d" % b, tag="hw%d" % b, align_bytes=64) for b in range(NB)]
-        hs = [keep.tile([P, BLK], U8, name="hs%d" % b, align_bytes=64) for b in range(NB)]
+        slot_w = {}
+        slot_s = [keep.tile([P, C], U8, name="slot_s%d" % e, align_bytes=64) for e in range(E)]
+        dh_by_slot = {}
+        dh_by_i = {}
+        dh_w = [keep.tile([P, GROUP], U32, name="dh_w%d" % b, tag="dh_w%d" % b, align_bytes=64) for b in range(GROUPS)]
+        dh_s = [keep.tile([P, GROUP], U8, name="dh_s%d" % b, align_bytes=64) for b in range(GROUPS)]
         window = keep.tile([P, T], F32, name="window", align_bytes=64)
-        res = [keep.tile([P, T // 2], F32, name="res%d" % h, align_bytes=64) for h in range(2)]
 
-        def offs_of(b):
-            return offsets[:, b * (BLK // 16) : (b + 1) * (BLK // 16)]
-
-        def gather(b, tag):
-            gw[b] = keep.tile([P, BLK], U32, name="gw%d" % b, tag=tag, align_bytes=64)
-            nc.vector.tensor_copy(gw[b][:], dyw[:].indirect(offs_of(b)))
-
-        def product(b, bank, i0, width):
-            e = b * BLK // C
-            acc = psum.tile([P, width], F32, name="acc_h", tag=bank)
-            nc.tensor.matmul_mx(
-                out=acc[:], lhsT=gw[b][:].bitcast(FP8X4), lhsT_scale=gs[e][:, b * BLK % C : b * BLK % C + BLK],
-                rhs=wbw[:, e, 2 * i0 : 2 * (i0 + width)].bitcast(FP4X4), rhs_scale=wbs[:, e, i0 : i0 + width],
-                start=True, stop=True,
-            )
-            dst = hb[b][:].rearrange("s (u p d) -> s u p d", u=2, d=2)[:, :, i0 // 4 : (i0 + width) // 4, :]
-            return dst, acc[:].rearrange("s (p u d) -> s u p d", u=2, d=2)
-
-        def first(b, tag, *banks):
-            hb[b] = keep.tile([P, H], BF16, name="hb%d" % b, tag=tag, align_bytes=64)
-            width = H // len(banks)
-            weight = g[:, b : b + 1]
-            dst, src = product(b, banks[0], 0, width)
-            nc.scalar.activation(out=dst, in_=src, func=COPY, scale=weight)
-            if len(banks) == 2:
-                dst, src = product(b, banks[1], width, width)
-                nc.vector.tensor_scalar(out=dst, in0=src, scalar1=weight, scalar2=None, op0=MULT)
-
-        def turn(b, bank):
-            pairs = hb[b][:].bitcast(F32)
-            turned = psum.tile([P, 2, BLK], F32, name="turned", tag=bank)
-            for u in range(2):
-                nc.tensor.transpose(turned[:, u, :], pairs[:, u * P : (u + 1) * P], ident[:])
-            dq[b] = keep.tile([P, 4 * BLK], BF16, name="dq%d" % b, tag="dq%d" % max(b, 1), align_bytes=64)
-            dst = dq[b][:].bitcast(F32).rearrange("p (s u) -> p s u", u=2)
-            src = turned[:].rearrange("p u s -> p s u")
-            if b < 2:
-                nc.vector.tensor_copy(out=dst, in_=src)
-            else:
-                nc.scalar.copy(out=dst, in_=src)
-
-        def quantise(b):
-            nc.vector.quantize_mx(out=hw[b][:].bitcast(FP8X4), scales=hs[b][:], in_=dq[b][:])
-
-        def second(b, bank, tag):
-            e = b * BLK // C
-            acc = psum.tile([P, BLK], F32, name="acc_x", tag=bank)
-            nc.tensor.matmul_mx(
-                out=acc[:], lhsT=waw[:, e, :].bitcast(FP4X4), lhsT_scale=was[:, e, :],
-                rhs=hw[b][:].bitcast(FP8X4), rhs_scale=hs[b][:], start=True, stop=True,
-            )
-            dx[b] = keep.tile([P, BLK], F32, name="dx%d" % b, tag=tag, align_bytes=64)
-            if b == 0:
-                nc.vector.tensor_copy(out=dx[b][:], in_=acc[:])
-            else:
-                nc.scalar.copy(out=dx[b][:], in_=acc[:])
-
-        def scatter(b):
-            nc.vector.tensor_copy(window[:].indirect(offs_of(b)), dx[b][:])
+        def offsets_of(slot0, slot1):
+            return offsets[:, slot0 // PER_COLUMN : slot1 // PER_COLUMN]
 
         def gather_scales(e):
-            nc.vector.tensor_copy(gs[e][:], dys[:].indirect(offsets[:, e * (C // 16) : (e + 1) * (C // 16)]))
+            nc.vector.tensor_copy(slot_s[e][:], dy_s[:].indirect(offsets_of(e * C, (e + 1) * C)))
 
+        def gather_words(b, tag):
+            slot_w[b] = keep.tile([P, GROUP], U32, name="slot_w%d" % b, tag=tag, align_bytes=64)
+            nc.vector.tensor_copy(slot_w[b][:], dy_w[:].indirect(offsets_of(b * GROUP, (b + 1) * GROUP)))
+
+        def first_pass(b, bank, i0, width):
+            e, s0 = divmod(b * GROUP, C)
+            sums = psum.tile([P, width], F32, name="sums_h", tag=bank)
+            nc.tensor.matmul_mx(
+                out=sums[:], lhsT=slot_w[b][:].bitcast(FP8X4), lhsT_scale=slot_s[e][:, s0 : s0 + GROUP],
+                rhs=wb_w[:, e, 2 * i0 : 2 * (i0 + width)].bitcast(FP4X4), rhs_scale=wb_s[:, e, i0 : i0 + width],
+                start=True, stop=True,
+            )
+            place = dh_by_slot[b][:].rearrange("s (u p v) -> s u p v", u=2, v=2)[:, :, i0 // 4 : (i0 + width) // 4, :]
+            return place, sums[:].rearrange("s (p u v) -> s u p v", u=2, v=2)
+
+        def first_product(b, tag, bank):
+            dh_by_slot[b] = keep.tile([P, H], BF16, name="dh_by_slot%d" % b, tag=tag, align_bytes=64)
+            place, sums = first_pass(b, bank, 0, H)
+            nc.scalar.activation(out=place, in_=sums, func=COPY, scale=gates[:, b : b + 1])
+
+        def first_product_shared(b, tag, scalar_bank, vector_bank):
+            dh_by_slot[b] = keep.tile([P, H], BF16, name="dh_by_slot%d" % b, tag=tag, align_bytes=64)
+            place, sums = first_pass(b, scalar_bank, 0, H // 2)
+            nc.scalar.activation(out=place, in_=sums, func=COPY, scale=gates[:, b : b + 1])
+            place, sums = first_pass(b, vector_bank, H // 2, H // 2)
+            nc.vector.tensor_scalar(out=place, in0=sums, scalar1=gates[:, b : b + 1], scalar2=None, op0=MULT)
+
+        def turn(b, bank, tag, copy):
+            pairs = dh_by_slot[b][:].bitcast(F32)
+            turned = psum.tile([P, 2, GROUP], F32, name="turned", tag=bank)
+            for u in range(2):
+                nc.tensor.transpose(turned[:, u, :], pairs[:, u * P : (u + 1) * P], identity[:])
+            dh_by_i[b] = keep.tile([P, 4 * GROUP], BF16, name="dh_by_i%d" % b, tag=tag, align_bytes=64)
+            copy(
+                out=dh_by_i[b][:].bitcast(F32).rearrange("p (s u) -> p s u", u=2),
+                in_=turned[:].rearrange("p u s -> p s u"),
+            )
+
+        def quantise(b):
+            nc.vector.quantize_mx(out=dh_w[b][:].bitcast(FP8X4), scales=dh_s[b][:], in_=dh_by_i[b][:])
+
+        def second_product(b, bank, dx, copy):
+            e = b * GROUP // C
+            sums = psum.tile([P, GROUP], F32, name="sums_x", tag=bank)
+            nc.tensor.matmul_mx(
+                out=sums[:], lhsT=wa_w[:, e, :].bitcast(FP4X4), lhsT_scale=wa_s[:, e, :],
+                rhs=dh_w[b][:].bitcast(FP8X4), rhs_scale=dh_s[b][:], start=True, stop=True,
+            )
+            copy(out=dx, in_=sums[:])
+
+        def scatter(b0, b1, dx):
+            nc.vector.tensor_copy(window[:].indirect(offsets_of(b0 * GROUP, b1 * GROUP)), dx)
+
+        on_vector, on_scalar = nc.vector.tensor_copy, nc.scalar.copy
         gather_scales(0)
-        gather(0, "gw0")
-        gather(1, "gw1")
+        gather_words(0, "slot_w0")
+        gather_words(1, "slot_w1")
         gather_scales(1)
-        gather(2, "gw2")
-        first(0, "hb0", "A", "B")
-        first(1, "hb1", "C")
-        first(2, "hb2", "D")
-        turn(0, "E")
-        gather(3, "hb0")
+        gather_words(2, "slot_w2")
+        first_product_shared(0, "dh_by_slot0", "A", "B")
+        first_product(1, "dh_by_slot1", "C")
+        first_product(2, "dh_by_slot2", "D")
+        turn(0, "E", "dh_by_i01", on_vector)
+        gather_words(3, "dh_by_slot0")
         quantise(0)
-        turn(1, "F")
-        second(0, "G", "dx0")
+        turn(1, "F", "dh_by_i01", on_vector)
+        dx0 = keep.tile([P, GROUP], F32, name="dx0", align_bytes=64)
+        second_product(0, "G", dx0[:], on_vector)
         quantise(1)
-        first(3, "hw0", "E")
-        turn(2, "G")
-        scatter(0)
+        first_product(3, "dh_w0", "E")
+        turn(2, "G", "dh_by_i2", on_scalar)
+        scatter(0, 1, dx0[:])
         quantise(2)
-        turn(3, "H")
-        second(1, "B", "hw0")
-        scatter(1)
+        turn(3, "H", "dh_by_i3", on_scalar)
+        dx1 = keep.tile([P, GROUP], F32, name="dx1", tag="dh_w0", align_bytes=64)
+        second_product(1, "B", dx1[:], on_scalar)
+        scatter(1, 2, dx1[:])
         quantise(3)
-        second(2, "H", "dx2")
-        second(3, "C", "dx3")
+        dx23 = keep.tile([P, 2 * GROUP], F32, name="dx23", align_bytes=64)
+        second_product(2, "H", dx23[:, :GROUP], on_scalar)
+        second_product(3, "C", dx23[:, GROUP:], on_scalar)
         base = psum.tile([P, T], F32, name="base", tag="B")
         nc.tensor.matmul_mx(
-            out=base[:], lhsT=wtw[:].bitcast(FP4X4), lhsT_scale=wts[:, 0, :],
-            rhs=dyw[:].bitcast(FP8X4), rhs_scale=dys[:], start=True, stop=True,
+            out=base[:], lhsT=wt_w[:].bitcast(FP4X4), lhsT_scale=wt_s[:, 0, :],
+            rhs=dy_w[:].bitcast(FP8X4), rhs_scale=dy_s[:], start=True, stop=True,
         )
-        scatter(2)
-        scatter(3)
-        for h, queue in enumerate((nc.sync, nc.scalar)):
-            cols = slice(h * (T // 2), (h + 1) * (T // 2))
-            nc.vector.tensor_tensor(out=res[h][:], in0=base[:, cols], in1=window[:, cols], op=ADD)
-            queue.dma_start(out=out[:, cols], in_=res[h][:])
+        scatter(2, 4, dx23[:])
+        for queue, cols in ((nc.sync, slice(0, FIRST_STORE)), (nc.scalar, slice(FIRST_STORE, T))):
+            result = keep.tile([P, cols.stop - cols.start], F32, name="result%d" % cols.start, align_bytes=64)
+            nc.vector.tensor_tensor(out=result[:], in0=base[:, cols], in1=window[:, cols], op=ADD)
+            queue.dma_start(out=out[:, cols], in_=result[:])

@@ -26,18 +26,18 @@ QUADRANTS = 4
 FIRST_STORE = 384
 
 
-def load_plane_filled(queue, plane, rows):
+def load_plane_filled(queues, plane, rows):
     words = rows.bitcast(I32)
     width = words.shape[1]
     for q in range(QUADRANTS):
         repeated = words[4 * q : 4 * q + 4, :].unsqueeze(0).broadcast_to([8, 4, width])
-        queue.dma_start(out=plane[32 * q : 32 * q + 32, :].bitcast(I32), in_=repeated)
+        queues[q % 2].dma_start(out=plane[32 * q : 32 * q + 32, :].bitcast(I32), in_=repeated)
 
 
-def load_planes(queue, planes, rows):
+def load_planes(queues, planes, rows):
     words = rows.bitcast(I32).rearrange("e c x -> c e x")
     for q in range(QUADRANTS):
-        queue.dma_start(out=planes[32 * q : 32 * q + 4, :, :].bitcast(I32), in_=words[4 * q : 4 * q + 4, :, :])
+        queues[q % len(queues)].dma_start(out=planes[32 * q : 32 * q + 4, :, :].bitcast(I32), in_=words[4 * q : 4 * q + 4, :, :])
 
 
 def tile_moe_adb_none_kernel(
@@ -53,49 +53,55 @@ def tile_moe_adb_none_kernel(
         dy_s = keep.tile([P, T], U8, name="dy_s", align_bytes=64)
         wb_w = keep.tile([P, E, 2 * H], U8, name="wb_w", align_bytes=64)
         wb_s = keep.tile([P, E, H], U8, name="wb_s", align_bytes=64)
+        wa_w = keep.tile([P, E, 2 * K], U8, name="wa_w", align_bytes=64)
         wa_s = keep.tile([P, E, K], U8, name="wa_s", align_bytes=64)
+        wt_w = keep.tile([P, 2 * K], U8, name="wt_w", align_bytes=64)
         wt_s = keep.tile([P, 1, K], U8, name="wt_s", align_bytes=64)
         gates = keep.tile([P, GROUPS], F32, name="gates")
         identity = keep.tile([P, P], F32, name="identity")
         warm_in = keep.tile([P, 1], F32, name="warm_in", tag="warm_in", align_bytes=64)
         warm_out = keep.tile([P, 1], BF16, name="warm_out", tag="warm_out", align_bytes=64)
 
-        for planes in (wb_s, wa_s, wt_s):
-            nc.vector.memset(planes[:].bitcast(I32), 0)
+        for cleared in (wb_s, wa_s, wt_s, wt_w):
+            nc.vector.memset(cleared[:].bitcast(I32), 0)
         nc.vector.memset(warm_in[:], 0.0)
-        nc.scalar.activation(out=warm_out[:], in_=warm_in[:], func=COPY)
-        make_identity(nc, identity[:])
-
-        nc.sync.dma_start(offsets[:], offs)
-        load_plane_filled(nc.sync, dy_s, dy_scales[0])
-        nc.sync.dma_start(out=dy_w[:].bitcast(I32), in_=dy_words[0].rearrange("p t d -> p (t d)").bitcast(I32))
-        wt_w = keep.tile([P, 2 * K], U8, name="wt_w", align_bytes=64)
-        nc.sync.dma_start(out=wt_w[:].bitcast(I32), in_=wt_words[0].bitcast(I32))
-        nc.sync.dma_start(
-            out=wb_w[:].bitcast(I32), in_=wbt_words[:, 0].rearrange("e p x -> p e x").bitcast(I32)
-        )
-        load_planes(nc.sync, wb_s, wbt_scales[:, 0])
-        with nc.allow_non_contiguous_dma(reason="one weight a slot, a slot a partition"):
-            nc.sync.dma_start(out=gates[:], in_=gate[0].rearrange("(b s) -> s b", s=GROUP))
-        load_planes(nc.sync, wa_s, wat_scales[:, 0])
-        wa_w = keep.tile([P, E, 2 * K], U8, name="wa_w", tag="warm_out", align_bytes=64)
-        nc.sync.dma_start(
+        nc.gpsimd.dma_start(
             out=wa_w[:].bitcast(I32), in_=wat_words[:, 0].rearrange("e p x -> p e x").bitcast(I32)
         )
+        make_identity(nc, identity[:])
+
+        wa_rows = wat_scales[:, 0].bitcast(I32).rearrange("e c x -> c e x")
+
+        def load_wa_rows(q):
+            nc.sync.dma_start(out=wa_s[32 * q : 32 * q + 4, :, :].bitcast(I32), in_=wa_rows[4 * q : 4 * q + 4, :, :])
+
+        nc.sync.dma_start(offsets[:], offs)
+        load_plane_filled((nc.scalar, nc.sync), dy_s, dy_scales[0])
+        nc.scalar.dma_start(out=dy_w[:].bitcast(I32), in_=dy_words[0].rearrange("p t d -> p (t d)").bitcast(I32))
+        nc.scalar.dma_start(out=wb_w[:].bitcast(I32), in_=wbt_words[:, 0].rearrange("e p x -> p e x").bitcast(I32))
+        with nc.allow_non_contiguous_dma(reason="one weight a slot, a slot a partition"):
+            nc.sync.dma_start(out=gates[:], in_=gate[0].rearrange("(b s) -> s b", s=GROUP))
+        load_planes((nc.sync, nc.scalar), wb_s, wbt_scales[:, 0])
+        nc.scalar.activation(out=warm_out[:], in_=warm_in[:], func=COPY)
+        load_wa_rows(0)
+        load_wa_rows(1)
+        load_wa_rows(2)
+        load_wa_rows(3)
         warm_sums = psum.tile([P, T], F32, name="warm_sums", tag="H")
         for width in (T, T // 2):
             nc.tensor.matmul_mx(
                 out=warm_sums[:, :width], lhsT=wt_w[:].bitcast(FP4X4), lhsT_scale=wt_s[:, 0, :],
                 rhs=dy_w[:, :width].bitcast(FP8X4), rhs_scale=dy_s[:, :width], start=True, stop=True,
             )
-        load_planes(nc.sync, wt_s, wt_scales)
+        nc.sync.dma_start(out=wt_w[:].bitcast(I32), in_=wt_words[0].bitcast(I32))
+        load_planes((nc.sync,), wt_s, wt_scales)
 
-        slot_w = {}
+        slot_w = [keep.tile([P, GROUP], U32, name="slot_w%d" % b, align_bytes=64) for b in range(GROUPS)]
         slot_s = [keep.tile([P, C], U8, name="slot_s%d" % e, align_bytes=64) for e in range(E)]
-        dh_by_slot = {}
-        dh_by_i = {}
-        dh_w = [keep.tile([P, GROUP], U32, name="dh_w%d" % b, tag="dh_w%d" % b, align_bytes=64) for b in range(GROUPS)]
-        dh_s = [keep.tile([P, GROUP], U8, name="dh_s%d" % b, align_bytes=64) for b in range(GROUPS)]
+        dh_by_slot = [keep.tile([P, H], BF16, name="dh_by_slot%d" % b, align_bytes=64) for b in range(GROUPS)]
+        dh_by_i = keep.tile([P, 4 * T], BF16, name="dh_by_i", align_bytes=64)
+        dh_w = keep.tile([P, T], U32, name="dh_w", align_bytes=64)
+        dh_s = keep.tile([P, T], U8, name="dh_s", align_bytes=64)
         window = keep.tile([P, T], F32, name="window", align_bytes=64)
 
         def offsets_of(slot0, slot1):
@@ -104,93 +110,91 @@ def tile_moe_adb_none_kernel(
         def gather_scales(e):
             nc.vector.tensor_copy(slot_s[e][:], dy_s[:].indirect(offsets_of(e * C, (e + 1) * C)))
 
-        def gather_words(b, tag):
-            slot_w[b] = keep.tile([P, GROUP], U32, name="slot_w%d" % b, tag=tag, align_bytes=64)
+        def gather_words(b):
             nc.vector.tensor_copy(slot_w[b][:], dy_w[:].indirect(offsets_of(b * GROUP, (b + 1) * GROUP)))
 
-        def first_pass(b, bank, i0, width):
+        def round_on_scalar(out, sums, weight):
+            nc.scalar.activation(out=out, in_=sums, func=COPY, scale=weight)
+
+        def round_on_vector(out, sums, weight):
+            nc.vector.tensor_scalar(out=out, in0=sums, scalar1=weight, scalar2=None, op0=MULT)
+
+        def first_product(b, banks):
             e, s0 = divmod(b * GROUP, C)
-            sums = psum.tile([P, width], F32, name="sums_h", tag=bank)
-            nc.tensor.matmul_mx(
-                out=sums[:], lhsT=slot_w[b][:].bitcast(FP8X4), lhsT_scale=slot_s[e][:, s0 : s0 + GROUP],
-                rhs=wb_w[:, e, 2 * i0 : 2 * (i0 + width)].bitcast(FP4X4), rhs_scale=wb_s[:, e, i0 : i0 + width],
-                start=True, stop=True,
-            )
-            place = dh_by_slot[b][:].rearrange("s (u p v) -> s u p v", u=2, v=2)[:, :, i0 // 4 : (i0 + width) // 4, :]
-            return place, sums[:].rearrange("s (p u v) -> s u p v", u=2, v=2)
+            place = dh_by_slot[b][:].rearrange("s (u p v) -> s u p v", u=2, v=2)
+            for half, gate_and_round in enumerate((round_on_scalar, round_on_vector)):
+                i0, i1 = half * H // 2, (half + 1) * H // 2
+                sums = psum.tile([P, H // 2], F32, name="sums_h", tag=banks[half])
+                nc.tensor.matmul_mx(
+                    out=sums[:], lhsT=slot_w[b][:].bitcast(FP8X4), lhsT_scale=slot_s[e][:, s0 : s0 + GROUP],
+                    rhs=wb_w[:, e, 2 * i0 : 2 * i1].bitcast(FP4X4), rhs_scale=wb_s[:, e, i0:i1], start=True, stop=True,
+                )
+                gate_and_round(
+                    place[:, :, i0 // 4 : i1 // 4, :],
+                    sums[:].rearrange("s (p u v) -> s u p v", u=2, v=2),
+                    gates[:, b : b + 1],
+                )
 
-        def first_product(b, tag, bank):
-            dh_by_slot[b] = keep.tile([P, H], BF16, name="dh_by_slot%d" % b, tag=tag, align_bytes=64)
-            place, sums = first_pass(b, bank, 0, H)
-            nc.scalar.activation(out=place, in_=sums, func=COPY, scale=gates[:, b : b + 1])
-
-        def first_product_shared(b, tag, scalar_bank, vector_bank):
-            dh_by_slot[b] = keep.tile([P, H], BF16, name="dh_by_slot%d" % b, tag=tag, align_bytes=64)
-            place, sums = first_pass(b, scalar_bank, 0, H // 2)
-            nc.scalar.activation(out=place, in_=sums, func=COPY, scale=gates[:, b : b + 1])
-            place, sums = first_pass(b, vector_bank, H // 2, H // 2)
-            nc.vector.tensor_scalar(out=place, in0=sums, scalar1=gates[:, b : b + 1], scalar2=None, op0=MULT)
-
-        def turn(b, bank, tag, copy):
+        def turn(b, bank, copy):
             pairs = dh_by_slot[b][:].bitcast(F32)
             turned = psum.tile([P, 2, GROUP], F32, name="turned", tag=bank)
             for u in range(2):
                 nc.tensor.transpose(turned[:, u, :], pairs[:, u * P : (u + 1) * P], identity[:])
-            dh_by_i[b] = keep.tile([P, 4 * GROUP], BF16, name="dh_by_i%d" % b, tag=tag, align_bytes=64)
             copy(
-                out=dh_by_i[b][:].bitcast(F32).rearrange("p (s u) -> p s u", u=2),
+                out=dh_by_i[:, 4 * b * GROUP : 4 * (b + 1) * GROUP].bitcast(F32).rearrange("p (s u) -> p s u", u=2),
                 in_=turned[:].rearrange("p u s -> p s u"),
             )
 
-        def quantise(b):
-            nc.vector.quantize_mx(out=dh_w[b][:].bitcast(FP8X4), scales=dh_s[b][:], in_=dh_by_i[b][:])
-
-        def second_product(b, bank, dx, copy):
-            e = b * GROUP // C
-            sums = psum.tile([P, GROUP], F32, name="sums_x", tag=bank)
-            nc.tensor.matmul_mx(
-                out=sums[:], lhsT=wa_w[:, e, :].bitcast(FP4X4), lhsT_scale=wa_s[:, e, :],
-                rhs=dh_w[b][:].bitcast(FP8X4), rhs_scale=dh_s[b][:], start=True, stop=True,
+        def quantise(b0, b1):
+            slots = slice(b0 * GROUP, b1 * GROUP)
+            nc.vector.quantize_mx(
+                out=dh_w[:, slots].bitcast(FP8X4), scales=dh_s[:, slots], in_=dh_by_i[:, 4 * slots.start : 4 * slots.stop]
             )
-            copy(out=dx, in_=sums[:])
+
+        def second_product(b0, b1, bank, copy):
+            sums = psum.tile([P, (b1 - b0) * GROUP], F32, name="sums_x", tag=bank)
+            for e in range(E):
+                slots = slice(max(b0 * GROUP, e * C), min(b1 * GROUP, (e + 1) * C))
+                if slots.start >= slots.stop:
+                    continue
+                nc.tensor.matmul_mx(
+                    out=sums[:, slots.start - b0 * GROUP : slots.stop - b0 * GROUP], lhsT=wa_w[:, e, :].bitcast(FP4X4), lhsT_scale=wa_s[:, e, :],
+                    rhs=dh_w[:, slots].bitcast(FP8X4), rhs_scale=dh_s[:, slots], start=True, stop=True,
+                )
+            dx = keep.tile([P, (b1 - b0) * GROUP], F32, name="dx%d" % b0, align_bytes=64)
+            copy(out=dx[:], in_=sums[:])
+            return dx
 
         def scatter(b0, b1, dx):
-            nc.vector.tensor_copy(window[:].indirect(offsets_of(b0 * GROUP, b1 * GROUP)), dx)
+            nc.vector.tensor_copy(window[:].indirect(offsets_of(b0 * GROUP, b1 * GROUP)), dx[:])
 
         on_vector, on_scalar = nc.vector.tensor_copy, nc.scalar.copy
         gather_scales(0)
-        gather_words(0, "slot_w0")
-        gather_words(1, "slot_w1")
         gather_scales(1)
-        gather_words(2, "slot_w2")
-        first_product_shared(0, "dh_by_slot0", "A", "B")
-        first_product(1, "dh_by_slot1", "C")
-        first_product(2, "dh_by_slot2", "D")
-        turn(0, "E", "dh_by_i01", on_vector)
-        gather_words(3, "dh_by_slot0")
-        quantise(0)
-        turn(1, "F", "dh_by_i01", on_vector)
-        dx0 = keep.tile([P, GROUP], F32, name="dx0", align_bytes=64)
-        second_product(0, "G", dx0[:], on_vector)
-        quantise(1)
-        first_product(3, "dh_w0", "E")
-        turn(2, "G", "dh_by_i2", on_scalar)
-        scatter(0, 1, dx0[:])
-        quantise(2)
-        turn(3, "H", "dh_by_i3", on_scalar)
-        dx1 = keep.tile([P, GROUP], F32, name="dx1", tag="dh_w0", align_bytes=64)
-        second_product(1, "B", dx1[:], on_scalar)
-        scatter(1, 2, dx1[:])
-        quantise(3)
-        dx23 = keep.tile([P, 2 * GROUP], F32, name="dx23", align_bytes=64)
-        second_product(2, "H", dx23[:, :GROUP], on_scalar)
-        second_product(3, "C", dx23[:, GROUP:], on_scalar)
-        base = psum.tile([P, T], F32, name="base", tag="B")
+        gather_words(0)
+        gather_words(1)
+        gather_words(2)
+        gather_words(3)
+        first_product(0, "AB")
+        first_product(1, "CD")
+        first_product(2, "EF")
+        first_product(3, "GH")
+        turn(0, "A", on_scalar)
+        quantise(0, 1)
+        turn(1, "B", on_vector)
+        turn(2, "C", on_scalar)
+        turn(3, "D", on_scalar)
+        dx_first = second_product(0, 1, "E", on_scalar)
+        quantise(1, 3)
+        quantise(3, 4)
+        scatter(0, 1, dx_first)
+        dx_rest = second_product(1, 4, "F", on_scalar)
+        base = psum.tile([P, T], F32, name="base", tag="F")
         nc.tensor.matmul_mx(
             out=base[:], lhsT=wt_w[:].bitcast(FP4X4), lhsT_scale=wt_s[:, 0, :],
             rhs=dy_w[:].bitcast(FP8X4), rhs_scale=dy_s[:], start=True, stop=True,
         )
-        scatter(2, 4, dx23[:])
+        scatter(1, 4, dx_rest)
         for queue, cols in ((nc.sync, slice(0, FIRST_STORE)), (nc.scalar, slice(FIRST_STORE, T))):
             result = keep.tile([P, cols.stop - cols.start], F32, name="result%d" % cols.start, align_bytes=64)
             nc.vector.tensor_tensor(out=result[:], in0=base[:, cols], in1=window[:, cols], op=ADD)

@@ -23,6 +23,7 @@ GROUP = 128
 GROUPS = T // GROUP
 PER_COLUMN = 16
 QUADRANTS = 4
+BLOCK = 32
 FIRST_STORE = 384
 
 
@@ -57,7 +58,8 @@ def tile_moe_adb_none_kernel(
         wa_s = keep.tile([P, E, K], U8, name="wa_s", align_bytes=64)
         wt_w = keep.tile([P, 2 * K], U8, name="wt_w", align_bytes=64)
         wt_s = keep.tile([P, 1, K], U8, name="wt_s", align_bytes=64)
-        gates = keep.tile([P, GROUPS], F32, name="gates")
+        gate_rows = keep.tile([P, BLOCK], F32, name="gate_rows", tag="slot_w", align_bytes=64)
+        gates = keep.tile([P, BLOCK], F32, name="gates", align_bytes=64)
         identity = keep.tile([P, P], F32, name="identity")
         warm_in = keep.tile([P, 1], F32, name="warm_in", tag="warm_in", align_bytes=64)
         warm_out = keep.tile([P, 1], BF16, name="warm_out", tag="warm_out", align_bytes=64)
@@ -77,10 +79,12 @@ def tile_moe_adb_none_kernel(
 
         nc.sync.dma_start(offsets[:], offs)
         load_plane_filled((nc.scalar, nc.sync), dy_s, dy_scales[0])
+        pitch = 2 * T + BLOCK // 4
+        spread = gate.rearrange("r c -> (r c)")[: 16 * pitch].rearrange("(u x) -> u x", x=pitch)[:, : 2 * T]
+        nc.sync.dma_start(out=gate_rows[:], in_=spread.rearrange("u (v a) -> u v a", a=GROUP)[:, :, :BLOCK])
+        nc.vector.transpose(gates[:], gate_rows[:])
         nc.scalar.dma_start(out=dy_w[:].bitcast(I32), in_=dy_words[0].rearrange("p t d -> p (t d)").bitcast(I32))
         nc.scalar.dma_start(out=wb_w[:].bitcast(I32), in_=wbt_words[:, 0].rearrange("e p x -> p e x").bitcast(I32))
-        with nc.allow_non_contiguous_dma(reason="one weight a slot, a slot a partition"):
-            nc.sync.dma_start(out=gates[:], in_=gate[0].rearrange("(b s) -> s b", s=GROUP))
         load_planes((nc.sync, nc.scalar), wb_s, wbt_scales[:, 0])
         nc.scalar.activation(out=warm_out[:], in_=warm_in[:], func=COPY)
         load_wa_rows(0)
@@ -96,7 +100,7 @@ def tile_moe_adb_none_kernel(
         nc.sync.dma_start(out=wt_w[:].bitcast(I32), in_=wt_words[0].bitcast(I32))
         load_planes((nc.sync,), wt_s, wt_scales)
 
-        slot_w = [keep.tile([P, GROUP], U32, name="slot_w%d" % b, align_bytes=64) for b in range(GROUPS)]
+        slot_w = keep.tile([P, T], U32, name="slot_w", tag="slot_w", align_bytes=64)
         slot_s = [keep.tile([P, C], U8, name="slot_s%d" % e, align_bytes=64) for e in range(E)]
         dh_by_slot = [keep.tile([P, H], BF16, name="dh_by_slot%d" % b, align_bytes=64) for b in range(GROUPS)]
         dh_by_i = keep.tile([P, 4 * T], BF16, name="dh_by_i", align_bytes=64)
@@ -111,7 +115,7 @@ def tile_moe_adb_none_kernel(
             nc.vector.tensor_copy(slot_s[e][:], dy_s[:].indirect(offsets_of(e * C, (e + 1) * C)))
 
         def gather_words(b):
-            nc.vector.tensor_copy(slot_w[b][:], dy_w[:].indirect(offsets_of(b * GROUP, (b + 1) * GROUP)))
+            nc.vector.tensor_copy(slot_w[:, b * GROUP : (b + 1) * GROUP], dy_w[:].indirect(offsets_of(b * GROUP, (b + 1) * GROUP)))
 
         def round_on_scalar(out, sums, weight):
             nc.scalar.activation(out=out, in_=sums, func=COPY, scale=weight)
@@ -126,7 +130,7 @@ def tile_moe_adb_none_kernel(
                 i0, i1 = half * H // 2, (half + 1) * H // 2
                 sums = psum.tile([P, H // 2], F32, name="sums_h", tag=banks[half])
                 nc.tensor.matmul_mx(
-                    out=sums[:], lhsT=slot_w[b][:].bitcast(FP8X4), lhsT_scale=slot_s[e][:, s0 : s0 + GROUP],
+                    out=sums[:], lhsT=slot_w[:, b * GROUP : (b + 1) * GROUP].bitcast(FP8X4), lhsT_scale=slot_s[e][:, s0 : s0 + GROUP],
                     rhs=wb_w[:, e, 2 * i0 : 2 * i1].bitcast(FP4X4), rhs_scale=wb_s[:, e, i0:i1], start=True, stop=True,
                 )
                 gate_and_round(

@@ -24,7 +24,8 @@ GROUPS = T // GROUP
 PER_COLUMN = 16
 QUADRANTS = 4
 BLOCK = 32
-FIRST_STORE = 384
+ALIGN = 64
+FIRST_STORE = 320
 
 
 def load_plane_filled(queues, plane, rows):
@@ -32,13 +33,21 @@ def load_plane_filled(queues, plane, rows):
     width = words.shape[1]
     for q in range(QUADRANTS):
         repeated = words[4 * q : 4 * q + 4, :].unsqueeze(0).broadcast_to([8, 4, width])
-        queues[q % 2].dma_start(out=plane[32 * q : 32 * q + 32, :].bitcast(I32), in_=repeated)
+        queues[q % len(queues)].dma_start(out=plane[32 * q : 32 * q + 32, :].bitcast(I32), in_=repeated)
 
 
 def load_planes(queues, planes, rows):
     words = rows.bitcast(I32).rearrange("e c x -> c e x")
     for q in range(QUADRANTS):
-        queues[q % len(queues)].dma_start(out=planes[32 * q : 32 * q + 4, :, :].bitcast(I32), in_=words[4 * q : 4 * q + 4, :, :])
+        queues[q % len(queues)].dma_start(
+            out=planes[32 * q : 32 * q + 4, :, :].bitcast(I32), in_=words[4 * q : 4 * q + 4, :, :]
+        )
+
+
+def gate_pieces(gate):
+    pitch = 2 * T + BLOCK // 4
+    spans = gate.rearrange("r c -> (r c)")[: 16 * pitch].rearrange("(u x) -> u x", x=pitch)[:, : 2 * T]
+    return spans.rearrange("u (v a) -> u v a", a=GROUP)[:, :, :BLOCK]
 
 
 def tile_moe_adb_none_kernel(
@@ -47,50 +56,44 @@ def tile_moe_adb_none_kernel(
     nc = tc.nc
     with ExitStack() as ctx:
         keep = ctx.enter_context(tc.tile_pool(name="keep", bufs=1))
+        laid = ctx.enter_context(tc.tile_pool(name="laid", bufs=1))
         psum = ctx.enter_context(tc.psum_pool(name="psum", bufs=1))
 
         offsets = keep.tile([P, T // PER_COLUMN], U16, name="offsets")
-        dy_w = keep.tile([P, T], U32, name="dy_w", align_bytes=64)
-        dy_s = keep.tile([P, T], U8, name="dy_s", align_bytes=64)
-        wb_w = keep.tile([P, E, 2 * H], U8, name="wb_w", align_bytes=64)
-        wb_s = keep.tile([P, E, H], U8, name="wb_s", align_bytes=64)
-        wa_w = keep.tile([P, E, 2 * K], U8, name="wa_w", align_bytes=64)
-        wa_s = keep.tile([P, E, K], U8, name="wa_s", align_bytes=64)
-        wt_w = keep.tile([P, 2 * K], U8, name="wt_w", align_bytes=64)
-        wt_s = keep.tile([P, 1, K], U8, name="wt_s", align_bytes=64)
-        gate_rows = keep.tile([P, BLOCK], F32, name="gate_rows", tag="slot_w", align_bytes=64)
-        gates = keep.tile([P, BLOCK], F32, name="gates", align_bytes=64)
+        dy_w = keep.tile([P, T], U32, name="dy_w", align_bytes=ALIGN)
+        dy_s = keep.tile([P, T], U8, name="dy_s", align_bytes=ALIGN)
+        wb_w = keep.tile([P, E, 2 * H], U8, name="wb_w", align_bytes=ALIGN)
+        wb_s = keep.tile([P, E, H], U8, name="wb_s", align_bytes=ALIGN)
+        wa_w = keep.tile([P, E, 2 * K], U8, name="wa_w", align_bytes=ALIGN)
+        wa_s = keep.tile([P, E, K], U8, name="wa_s", align_bytes=ALIGN)
+        wt_w = keep.tile([P, 2 * K], U8, name="wt_w", align_bytes=ALIGN)
+        wt_s = keep.tile([P, 1, K], U8, name="wt_s", align_bytes=ALIGN)
+        gate_runs = laid.tile([P, BLOCK], F32, name="gate_runs", align_bytes=ALIGN, offset=C - ALIGN)
+        gates = keep.tile([P, BLOCK], F32, name="gates", align_bytes=ALIGN)
         identity = keep.tile([P, P], F32, name="identity")
-        warm_in = keep.tile([P, 1], F32, name="warm_in", tag="warm_in", align_bytes=64)
-        warm_out = keep.tile([P, 1], BF16, name="warm_out", tag="warm_out", align_bytes=64)
+        warm_in = keep.tile([P, 1], F32, name="warm_in", align_bytes=ALIGN)
+        warm_out = keep.tile([P, 1], BF16, name="warm_out", align_bytes=ALIGN)
 
-        for cleared in (wb_s, wa_s, wt_s, wt_w):
-            nc.vector.memset(cleared[:].bitcast(I32), 0)
+        for planes in (wb_s, wa_s, wt_s):
+            nc.vector.memset(planes[:].bitcast(I32), 0)
+        nc.vector.memset(wt_w[:].bitcast(I32), 0)
         nc.vector.memset(warm_in[:], 0.0)
         nc.gpsimd.dma_start(
             out=wa_w[:].bitcast(I32), in_=wat_words[:, 0].rearrange("e p x -> p e x").bitcast(I32)
         )
         make_identity(nc, identity[:])
 
-        wa_rows = wat_scales[:, 0].bitcast(I32).rearrange("e c x -> c e x")
-
-        def load_wa_rows(q):
-            nc.sync.dma_start(out=wa_s[32 * q : 32 * q + 4, :, :].bitcast(I32), in_=wa_rows[4 * q : 4 * q + 4, :, :])
-
         nc.sync.dma_start(offsets[:], offs)
         load_plane_filled((nc.scalar, nc.sync), dy_s, dy_scales[0])
-        pitch = 2 * T + BLOCK // 4
-        spread = gate.rearrange("r c -> (r c)")[: 16 * pitch].rearrange("(u x) -> u x", x=pitch)[:, : 2 * T]
-        nc.sync.dma_start(out=gate_rows[:], in_=spread.rearrange("u (v a) -> u v a", a=GROUP)[:, :, :BLOCK])
-        nc.vector.transpose(gates[:], gate_rows[:])
+        nc.sync.dma_start(out=gate_runs[:], in_=gate_pieces(gate))
+        nc.vector.transpose(gates[:], gate_runs[:])
         nc.scalar.dma_start(out=dy_w[:].bitcast(I32), in_=dy_words[0].rearrange("p t d -> p (t d)").bitcast(I32))
-        nc.scalar.dma_start(out=wb_w[:].bitcast(I32), in_=wbt_words[:, 0].rearrange("e p x -> p e x").bitcast(I32))
+        nc.scalar.dma_start(
+            out=wb_w[:].bitcast(I32), in_=wbt_words[:, 0].rearrange("e p x -> p e x").bitcast(I32)
+        )
         load_planes((nc.sync, nc.scalar), wb_s, wbt_scales[:, 0])
         nc.scalar.activation(out=warm_out[:], in_=warm_in[:], func=COPY)
-        load_wa_rows(0)
-        load_wa_rows(1)
-        load_wa_rows(2)
-        load_wa_rows(3)
+        load_planes((nc.sync,), wa_s, wat_scales[:, 0])
         warm_sums = psum.tile([P, T], F32, name="warm_sums", tag="H")
         for width in (T, T // 2):
             nc.tensor.matmul_mx(
@@ -100,22 +103,29 @@ def tile_moe_adb_none_kernel(
         nc.sync.dma_start(out=wt_w[:].bitcast(I32), in_=wt_words[0].bitcast(I32))
         load_planes((nc.sync,), wt_s, wt_scales)
 
-        slot_w = keep.tile([P, T], U32, name="slot_w", tag="slot_w", align_bytes=64)
-        slot_s = [keep.tile([P, C], U8, name="slot_s%d" % e, align_bytes=64) for e in range(E)]
-        dh_by_slot = [keep.tile([P, H], BF16, name="dh_by_slot%d" % b, align_bytes=64) for b in range(GROUPS)]
-        dh_by_i = keep.tile([P, 4 * T], BF16, name="dh_by_i", align_bytes=64)
-        dh_w = keep.tile([P, T], U32, name="dh_w", align_bytes=64)
-        dh_s = keep.tile([P, T], U8, name="dh_s", align_bytes=64)
-        window = keep.tile([P, T], F32, name="window", align_bytes=64)
+        slot_w = laid.tile([P, T], U32, name="slot_w", align_bytes=ALIGN, offset=C)
+        slot_s = [
+            keep.tile([P, C], U8, name="slot_s0", align_bytes=ALIGN),
+            laid.tile([P, C], U8, name="slot_s1", align_bytes=ALIGN, offset=0),
+        ]
+        dh_by_slot = [keep.tile([P, H], BF16, name="dh_by_slot%d" % b, align_bytes=ALIGN) for b in range(GROUPS)]
+        dh_by_i = keep.tile([P, 4 * T], BF16, name="dh_by_i", align_bytes=ALIGN)
+        dh_w = keep.tile([P, T], U32, name="dh_w", align_bytes=ALIGN)
+        dh_s = keep.tile([P, T], U8, name="dh_s", align_bytes=ALIGN)
+        window = keep.tile([P, T], F32, name="window", align_bytes=ALIGN)
 
-        def offsets_of(slot0, slot1):
-            return offsets[:, slot0 // PER_COLUMN : slot1 // PER_COLUMN]
+        def slots_of(b0, b1):
+            return slice(b0 * GROUP, b1 * GROUP)
+
+        def offsets_of(slots):
+            return offsets[:, slots.start // PER_COLUMN : slots.stop // PER_COLUMN]
 
         def gather_scales(e):
-            nc.vector.tensor_copy(slot_s[e][:], dy_s[:].indirect(offsets_of(e * C, (e + 1) * C)))
+            nc.vector.tensor_copy(slot_s[e][:], dy_s[:].indirect(offsets_of(slice(e * C, (e + 1) * C))))
 
         def gather_words(b):
-            nc.vector.tensor_copy(slot_w[:, b * GROUP : (b + 1) * GROUP], dy_w[:].indirect(offsets_of(b * GROUP, (b + 1) * GROUP)))
+            slots = slots_of(b, b + 1)
+            nc.vector.tensor_copy(slot_w[:, slots], dy_w[:].indirect(offsets_of(slots)))
 
         def round_on_scalar(out, sums, weight):
             nc.scalar.activation(out=out, in_=sums, func=COPY, scale=weight)
@@ -130,8 +140,10 @@ def tile_moe_adb_none_kernel(
                 i0, i1 = half * H // 2, (half + 1) * H // 2
                 sums = psum.tile([P, H // 2], F32, name="sums_h", tag=banks[half])
                 nc.tensor.matmul_mx(
-                    out=sums[:], lhsT=slot_w[:, b * GROUP : (b + 1) * GROUP].bitcast(FP8X4), lhsT_scale=slot_s[e][:, s0 : s0 + GROUP],
-                    rhs=wb_w[:, e, 2 * i0 : 2 * i1].bitcast(FP4X4), rhs_scale=wb_s[:, e, i0:i1], start=True, stop=True,
+                    out=sums[:],
+                    lhsT=slot_w[:, slots_of(b, b + 1)].bitcast(FP8X4), lhsT_scale=slot_s[e][:, s0 : s0 + GROUP],
+                    rhs=wb_w[:, e, 2 * i0 : 2 * i1].bitcast(FP4X4), rhs_scale=wb_s[:, e, i0:i1],
+                    start=True, stop=True,
                 )
                 gate_and_round(
                     place[:, :, i0 // 4 : i1 // 4, :],
@@ -150,49 +162,46 @@ def tile_moe_adb_none_kernel(
             )
 
         def quantise(b0, b1):
-            slots = slice(b0 * GROUP, b1 * GROUP)
+            slots = slots_of(b0, b1)
             nc.vector.quantize_mx(
-                out=dh_w[:, slots].bitcast(FP8X4), scales=dh_s[:, slots], in_=dh_by_i[:, 4 * slots.start : 4 * slots.stop]
+                out=dh_w[:, slots].bitcast(FP8X4), scales=dh_s[:, slots],
+                in_=dh_by_i[:, 4 * slots.start : 4 * slots.stop],
             )
 
-        def second_product(b0, b1, bank, copy):
+        def second_product(b0, b1, bank, dx):
             sums = psum.tile([P, (b1 - b0) * GROUP], F32, name="sums_x", tag=bank)
-            for e in range(E):
-                slots = slice(max(b0 * GROUP, e * C), min(b1 * GROUP, (e + 1) * C))
-                if slots.start >= slots.stop:
-                    continue
+            for b in range(b0, b1):
+                e = b * GROUP // C
+                slots = slots_of(b, b + 1)
                 nc.tensor.matmul_mx(
-                    out=sums[:, slots.start - b0 * GROUP : slots.stop - b0 * GROUP], lhsT=wa_w[:, e, :].bitcast(FP4X4), lhsT_scale=wa_s[:, e, :],
+                    out=sums[:, slots_of(b - b0, b - b0 + 1)],
+                    lhsT=wa_w[:, e, :].bitcast(FP4X4), lhsT_scale=wa_s[:, e, :],
                     rhs=dh_w[:, slots].bitcast(FP8X4), rhs_scale=dh_s[:, slots], start=True, stop=True,
                 )
-            dx = keep.tile([P, (b1 - b0) * GROUP], F32, name="dx%d" % b0, align_bytes=64)
-            copy(out=dx[:], in_=sums[:])
-            return dx
+            nc.scalar.copy(out=dx, in_=sums[:])
 
         def scatter(b0, b1, dx):
-            nc.vector.tensor_copy(window[:].indirect(offsets_of(b0 * GROUP, b1 * GROUP)), dx[:])
+            nc.vector.tensor_copy(window[:].indirect(offsets_of(slots_of(b0, b1))), dx[:])
 
-        on_vector, on_scalar = nc.vector.tensor_copy, nc.scalar.copy
-        gather_scales(0)
-        gather_scales(1)
-        gather_words(0)
-        gather_words(1)
-        gather_words(2)
-        gather_words(3)
-        first_product(0, "AB")
-        first_product(1, "CD")
-        first_product(2, "EF")
-        first_product(3, "GH")
-        turn(0, "A", on_scalar)
+        for e in range(E):
+            gather_scales(e)
+            for b in range(e * C // GROUP, (e + 1) * C // GROUP):
+                gather_words(b)
+        for b, banks in enumerate(("AB", "CD", "EF", "GH")):
+            first_product(b, banks)
+        turn(0, "A", nc.scalar.copy)
         quantise(0, 1)
-        turn(1, "B", on_vector)
-        turn(2, "C", on_scalar)
-        turn(3, "D", on_scalar)
-        dx_first = second_product(0, 1, "E", on_scalar)
+        turn(1, "B", nc.vector.tensor_copy)
+        turn(2, "C", nc.scalar.copy)
+        turn(3, "D", nc.scalar.copy)
+        dx_first = keep.tile([P, GROUP], F32, name="dx_first", align_bytes=ALIGN)
+        dx_rest = keep.tile([P, T - GROUP], F32, name="dx_rest", align_bytes=ALIGN)
+        second_product(0, 1, "E", dx_first[:])
         quantise(1, 3)
         quantise(3, 4)
         scatter(0, 1, dx_first)
-        dx_rest = second_product(1, 4, "F", on_scalar)
+        second_product(1, 3, "G", dx_rest[:, : 2 * GROUP])
+        second_product(3, 4, "F", dx_rest[:, 2 * GROUP :])
         base = psum.tile([P, T], F32, name="base", tag="F")
         nc.tensor.matmul_mx(
             out=base[:], lhsT=wt_w[:].bitcast(FP4X4), lhsT_scale=wt_s[:, 0, :],
@@ -200,6 +209,6 @@ def tile_moe_adb_none_kernel(
         )
         scatter(1, 4, dx_rest)
         for queue, cols in ((nc.sync, slice(0, FIRST_STORE)), (nc.scalar, slice(FIRST_STORE, T))):
-            result = keep.tile([P, cols.stop - cols.start], F32, name="result%d" % cols.start, align_bytes=64)
+            result = keep.tile([P, cols.stop - cols.start], F32, name="result%d" % cols.start, align_bytes=ALIGN)
             nc.vector.tensor_tensor(out=result[:], in0=base[:, cols], in1=window[:, cols], op=ADD)
             queue.dma_start(out=out[:, cols], in_=result[:])

@@ -71,13 +71,10 @@ def tile_moe_adb_none_kernel(
         gate_runs = laid.tile([P, BLOCK], F32, name="gate_runs", align_bytes=ALIGN, offset=C - ALIGN)
         gates = keep.tile([P, BLOCK], F32, name="gates", align_bytes=ALIGN)
         identity = keep.tile([P, P], F32, name="identity")
-        warm_in = keep.tile([P, 1], F32, name="warm_in", align_bytes=ALIGN)
-        warm_out = keep.tile([P, 1], BF16, name="warm_out", align_bytes=ALIGN)
 
         for planes in (wb_s, wa_s, wt_s):
             nc.vector.memset(planes[:].bitcast(I32), 0)
         nc.vector.memset(wt_w[:].bitcast(I32), 0)
-        nc.vector.memset(warm_in[:], 0.0)
         nc.gpsimd.dma_start(
             out=wa_w[:].bitcast(I32), in_=wat_words[:, 0].rearrange("e p x -> p e x").bitcast(I32)
         )
@@ -92,7 +89,6 @@ def tile_moe_adb_none_kernel(
             out=wb_w[:].bitcast(I32), in_=wbt_words[:, 0].rearrange("e p x -> p e x").bitcast(I32)
         )
         load_planes((nc.sync, nc.scalar), wb_s, wbt_scales[:, 0])
-        nc.scalar.activation(out=warm_out[:], in_=warm_in[:], func=COPY)
         load_planes((nc.sync,), wa_s, wat_scales[:, 0])
         warm_sums = psum.tile([P, T], F32, name="warm_sums", tag="H")
         for width in (T, T // 2):

@@ -75,6 +75,10 @@ def tile_moe_adb_none_kernel(
         for planes in (wb_s, wa_s, wt_s):
             nc.vector.memset(planes[:].bitcast(I32), 0)
         nc.vector.memset(wt_w[:].bitcast(I32), 0)
+        window_first = keep.tile([P, T], F32, name="window_first", align_bytes=ALIGN)
+        window_rest = keep.tile([P, T], F32, name="window_rest", align_bytes=ALIGN)
+        for window in (window_first, window_rest):
+            nc.vector.memset(window[:], 0.0)
         nc.gpsimd.dma_start(
             out=wa_w[:].bitcast(I32), in_=wat_words[:, 0].rearrange("e p x -> p e x").bitcast(I32)
         )
@@ -108,7 +112,6 @@ def tile_moe_adb_none_kernel(
         dh_by_i = keep.tile([P, 4 * T], BF16, name="dh_by_i", align_bytes=ALIGN)
         dh_w = keep.tile([P, T], U32, name="dh_w", align_bytes=ALIGN)
         dh_s = keep.tile([P, T], U8, name="dh_s", align_bytes=ALIGN)
-        window = keep.tile([P, T], F32, name="window", align_bytes=ALIGN)
 
         def slots_of(b0, b1):
             return slice(b0 * GROUP, b1 * GROUP)
@@ -176,7 +179,7 @@ def tile_moe_adb_none_kernel(
                 )
             nc.scalar.copy(out=dx, in_=sums[:])
 
-        def scatter(b0, b1, dx):
+        def scatter(window, b0, b1, dx):
             nc.vector.tensor_copy(window[:].indirect(offsets_of(slots_of(b0, b1))), dx[:])
 
         for e in range(E):
@@ -195,16 +198,20 @@ def tile_moe_adb_none_kernel(
         second_product(0, 1, "E", dx_first[:])
         quantise(1, 3)
         quantise(3, 4)
-        scatter(0, 1, dx_first)
+        scatter(window_first, 0, 1, dx_first)
         second_product(1, 3, "G", dx_rest[:, : 2 * GROUP])
         second_product(3, 4, "F", dx_rest[:, 2 * GROUP :])
-        base = psum.tile([P, T], F32, name="base", tag="F")
+        base = psum.tile([P, T], F32, name="base", tag="G")
         nc.tensor.matmul_mx(
             out=base[:], lhsT=wt_w[:].bitcast(FP4X4), lhsT_scale=wt_s[:, 0, :],
             rhs=dy_w[:].bitcast(FP8X4), rhs_scale=dy_s[:], start=True, stop=True,
         )
-        scatter(1, 4, dx_rest)
+        scatter(window_rest, 1, 4, dx_rest)
+        base_rows = keep.tile([P, T], F32, name="base_rows", align_bytes=ALIGN)
+        nc.scalar.copy(out=base_rows[:], in_=base[:])
+        partial = keep.tile([P, T], F32, name="partial", align_bytes=ALIGN)
+        nc.gpsimd.tensor_tensor(out=partial[:], in0=base_rows[:], in1=window_first[:], op=ADD)
         for queue, cols in ((nc.sync, slice(0, FIRST_STORE)), (nc.scalar, slice(FIRST_STORE, T))):
             result = keep.tile([P, cols.stop - cols.start], F32, name="result%d" % cols.start, align_bytes=ALIGN)
-            nc.vector.tensor_tensor(out=result[:], in0=base[:, cols], in1=window[:, cols], op=ADD)
+            nc.vector.tensor_tensor(out=result[:], in0=partial[:, cols], in1=window_rest[:, cols], op=ADD)
             queue.dma_start(out=out[:, cols], in_=result[:])

@@ -194,19 +194,22 @@ def tile_moe_adb_none_kernel(
         turn(2, "C", nc.scalar.copy)
         turn(3, "D", nc.scalar.copy)
         dx_first = keep.tile([P, GROUP], F32, name="dx_first", align_bytes=ALIGN)
-        dx_rest = keep.tile([P, T - GROUP], F32, name="dx_rest", align_bytes=ALIGN)
+        dx_second = keep.tile([P, GROUP], F32, name="dx_second", align_bytes=ALIGN)
+        dx_rest = keep.tile([P, C], F32, name="dx_rest", align_bytes=ALIGN)
         second_product(0, 1, "E", dx_first[:])
         quantise(1, 3)
         quantise(3, 4)
-        scatter(window_first, 0, 1, dx_first)
-        second_product(1, 3, "G", dx_rest[:, : 2 * GROUP])
-        second_product(3, 4, "F", dx_rest[:, 2 * GROUP :])
+        scatter(window_rest, 0, 1, dx_first)
+        second_product(1, 2, "G", dx_second[:])
+        scatter(window_first, 1, 2, dx_second)
+        second_product(2, 3, "H", dx_rest[:, :GROUP])
+        second_product(3, 4, "F", dx_rest[:, GROUP:])
         base = psum.tile([P, T], F32, name="base", tag="G")
         nc.tensor.matmul_mx(
             out=base[:], lhsT=wt_w[:].bitcast(FP4X4), lhsT_scale=wt_s[:, 0, :],
             rhs=dy_w[:].bitcast(FP8X4), rhs_scale=dy_s[:], start=True, stop=True,
         )
-        scatter(window_rest, 1, 4, dx_rest)
+        scatter(window_rest, 2, 4, dx_rest)
         base_rows = keep.tile([P, T], F32, name="base_rows", align_bytes=ALIGN)
         nc.scalar.copy(out=base_rows[:], in_=base[:])
         partial = keep.tile([P, T], F32, name="partial", align_bytes=ALIGN)

@@ -204,16 +204,18 @@ def tile_moe_adb_none_kernel(
         scatter(window_first, 1, 2, dx_second)
         second_product(2, 3, "H", dx_rest[:, :GROUP])
         second_product(3, 4, "F", dx_rest[:, GROUP:])
-        base = psum.tile([P, T], F32, name="base", tag="G")
+        base = psum.tile([P, T], F32, name="base", tag="F")
         nc.tensor.matmul_mx(
             out=base[:], lhsT=wt_w[:].bitcast(FP4X4), lhsT_scale=wt_s[:, 0, :],
             rhs=dy_w[:].bitcast(FP8X4), rhs_scale=dy_s[:], start=True, stop=True,
         )
         scatter(window_rest, 2, 4, dx_rest)
-        base_rows = keep.tile([P, T], F32, name="base_rows", align_bytes=ALIGN)
-        nc.scalar.copy(out=base_rows[:], in_=base[:])
+        head, tail = slice(0, FIRST_STORE), slice(FIRST_STORE, T)
+        base_rows = keep.tile([P, FIRST_STORE], F32, name="base_rows", align_bytes=ALIGN)
+        nc.scalar.copy(out=base_rows[:], in_=base[:, head])
         partial = keep.tile([P, T], F32, name="partial", align_bytes=ALIGN)
-        nc.gpsimd.tensor_tensor(out=partial[:], in0=base_rows[:], in1=window_first[:], op=ADD)
+        nc.gpsimd.tensor_tensor(out=partial[:, head], in0=base_rows[:], in1=window_first[:, head], op=ADD)
+        nc.vector.tensor_tensor(out=partial[:, tail], in0=base[:, tail], in1=window_first[:, tail], op=ADD)
         for queue, cols in ((nc.sync, slice(0, FIRST_STORE)), (nc.scalar, slice(FIRST_STORE, T))):
             result = keep.tile([P, cols.stop - cols.start], F32, name="result%d" % cols.start, align_bytes=ALIGN)
             nc.vector.tensor_tensor(out=result[:], in0=partial[:, cols], in1=window_rest[:, cols], op=ADD)

@@ -74,11 +74,11 @@ def tile_moe_adb_none_kernel(
 
         for planes in (wb_s, wa_s, wt_s):
             nc.vector.memset(planes[:].bitcast(I32), 0)
-        nc.vector.memset(wt_w[:].bitcast(I32), 0)
         window_first = keep.tile([P, T], F32, name="window_first", align_bytes=ALIGN)
         window_rest = keep.tile([P, T], F32, name="window_rest", align_bytes=ALIGN)
         for window in (window_first, window_rest):
             nc.vector.memset(window[:], 0.0)
+        nc.gpsimd.dma_start(out=wt_w[:].bitcast(I32), in_=wt_words[0].bitcast(I32))
         nc.gpsimd.dma_start(
             out=wa_w[:].bitcast(I32), in_=wat_words[:, 0].rearrange("e p x -> p e x").bitcast(I32)
         )
@@ -94,13 +94,6 @@ def tile_moe_adb_none_kernel(
         )
         load_planes((nc.sync, nc.scalar), wb_s, wbt_scales[:, 0])
         load_planes((nc.sync,), wa_s, wat_scales[:, 0])
-        warm_sums = psum.tile([P, T], F32, name="warm_sums", tag="H")
-        for width in (T, T // 2):
-            nc.tensor.matmul_mx(
-                out=warm_sums[:, :width], lhsT=wt_w[:].bitcast(FP4X4), lhsT_scale=wt_s[:, 0, :],
-                rhs=dy_w[:, :width].bitcast(FP8X4), rhs_scale=dy_s[:, :width], start=True, stop=True,
-            )
-        nc.sync.dma_start(out=wt_w[:].bitcast(I32), in_=wt_words[0].bitcast(I32))
         load_planes((nc.sync,), wt_s, wt_scales)
 
         slot_w = laid.tile([P, T], U32, name="slot_w", align_bytes=ALIGN, offset=C)
@@ -167,20 +160,23 @@ def tile_moe_adb_none_kernel(
                 in_=dh_by_i[:, 4 * slots.start : 4 * slots.stop],
             )
 
-        def second_product(b0, b1, bank, dx):
-            sums = psum.tile([P, (b1 - b0) * GROUP], F32, name="sums_x", tag=bank)
-            for b in range(b0, b1):
-                e = b * GROUP // C
-                slots = slots_of(b, b + 1)
+        def second_product(b0, b1, bank, dx, copy, tokens=None):
+            slots = slots_of(b0, b1)
+            width = slots.stop - slots.start
+            sums = psum.tile([P, T], F32, name="sums_x", tag=bank)
+            e = b0 * GROUP // C
+            nc.tensor.matmul_mx(
+                out=sums[:, :width],
+                lhsT=wa_w[:, e, :].bitcast(FP4X4), lhsT_scale=wa_s[:, e, :],
+                rhs=dh_w[:, slots].bitcast(FP8X4), rhs_scale=dh_s[:, slots], start=True, stop=True,
+            )
+            if tokens is not None:
                 nc.tensor.matmul_mx(
-                    out=sums[:, slots_of(b - b0, b - b0 + 1)],
-                    lhsT=wa_w[:, e, :].bitcast(FP4X4), lhsT_scale=wa_s[:, e, :],
-                    rhs=dh_w[:, slots].bitcast(FP8X4), rhs_scale=dh_s[:, slots], start=True, stop=True,
+                    out=sums[:, C:], lhsT=wt_w[:].bitcast(FP4X4), lhsT_scale=wt_s[:, 0, :],
+                    rhs=dy_w[:, tokens].bitcast(FP8X4), rhs_scale=dy_s[:, tokens], start=True, stop=True,
                 )
-            nc.scalar.copy(out=dx, in_=sums[:])
-
-        def scatter(window, b0, b1, dx):
-            nc.vector.tensor_copy(window[:].indirect(offsets_of(slots_of(b0, b1))), dx[:])
+            copy(out=dx, in_=sums[:, :width])
+            return sums[:, C:]
 
         for e in range(E):
             gather_scales(e)
@@ -188,35 +184,30 @@ def tile_moe_adb_none_kernel(
                 gather_words(b)
         for b, banks in enumerate(("AB", "CD", "EF", "GH")):
             first_product(b, banks)
-        turn(0, "A", nc.scalar.copy)
+        turn(0, "A", nc.vector.tensor_copy)
         quantise(0, 1)
-        turn(1, "B", nc.vector.tensor_copy)
+        turn(1, "B", nc.scalar.copy)
+        quantise(1, 2)
         turn(2, "C", nc.scalar.copy)
+        quantise(2, 3)
         turn(3, "D", nc.scalar.copy)
-        dx_first = keep.tile([P, GROUP], F32, name="dx_first", align_bytes=ALIGN)
-        dx_second = keep.tile([P, GROUP], F32, name="dx_second", align_bytes=ALIGN)
-        dx_rest = keep.tile([P, C], F32, name="dx_rest", align_bytes=ALIGN)
-        second_product(0, 1, "E", dx_first[:])
-        quantise(1, 3)
         quantise(3, 4)
-        scatter(window_rest, 0, 1, dx_first)
-        second_product(1, 2, "G", dx_second[:])
-        scatter(window_first, 1, 2, dx_second)
-        second_product(2, 3, "H", dx_rest[:, :GROUP])
-        second_product(3, 4, "F", dx_rest[:, GROUP:])
-        base = psum.tile([P, T], F32, name="base", tag="F")
-        nc.tensor.matmul_mx(
-            out=base[:], lhsT=wt_w[:].bitcast(FP4X4), lhsT_scale=wt_s[:, 0, :],
-            rhs=dy_w[:].bitcast(FP8X4), rhs_scale=dy_s[:], start=True, stop=True,
-        )
-        scatter(window_rest, 2, 4, dx_rest)
-        head, tail = slice(0, FIRST_STORE), slice(FIRST_STORE, T)
-        base_rows = keep.tile([P, FIRST_STORE], F32, name="base_rows", align_bytes=ALIGN)
-        nc.scalar.copy(out=base_rows[:], in_=base[:, head])
+        dx = [keep.tile([P, GROUP], F32, name="dx%d" % b, align_bytes=ALIGN) for b in range(GROUPS)]
+        second_product(0, 1, "E", dx[0][:], nc.scalar.copy)
+        second_product(1, 2, "F", dx[1][:], nc.scalar.copy)
+        nc.vector.tensor_copy(window_rest[:].indirect(offsets_of(slots_of(0, 1))), dx[0][:])
+        nc.scalar.activation(out=window_first[:].indirect(offsets_of(slots_of(1, 2))), in_=dx[1][:], func=COPY)
+        stores = ((nc.sync, slice(0, C)), (nc.scalar, slice(C, T)))
+        base = [
+            second_product(2, 3, "G", dx[2][:], nc.scalar.copy, stores[0][1]),
+            second_product(3, 4, "H", dx[3][:], nc.vector.tensor_copy, stores[1][1]),
+        ]
+        nc.scalar.activation(out=window_first[:].indirect(offsets_of(slots_of(2, 3))), in_=dx[2][:], func=COPY)
+        nc.vector.tensor_copy(window_rest[:].indirect(offsets_of(slots_of(3, 4))), dx[3][:])
         partial = keep.tile([P, T], F32, name="partial", align_bytes=ALIGN)
-        nc.gpsimd.tensor_tensor(out=partial[:, head], in0=base_rows[:], in1=window_first[:, head], op=ADD)
-        nc.vector.tensor_tensor(out=partial[:, tail], in0=base[:, tail], in1=window_first[:, tail], op=ADD)
-        for queue, cols in ((nc.sync, slice(0, FIRST_STORE)), (nc.scalar, slice(FIRST_STORE, T))):
+        for half, (queue, cols) in enumerate(stores):
+            nc.vector.tensor_tensor(out=partial[:, cols], in0=base[half], in1=window_rest[:, cols], op=ADD)
+        for queue, cols in stores:
             result = keep.tile([P, cols.stop - cols.start], F32, name="result%d" % cols.start, align_bytes=ALIGN)
-            nc.vector.tensor_tensor(out=result[:], in0=partial[:, cols], in1=window_rest[:, cols], op=ADD)
+            nc.vector.tensor_tensor(out=result[:], in0=partial[:, cols], in1=window_first[:, cols], op=ADD)
             queue.dma_start(out=out[:, cols], in_=result[:])

@@ -78,7 +78,6 @@ def tile_moe_adb_none_kernel(
         window_rest = keep.tile([P, T], F32, name="window_rest", align_bytes=ALIGN)
         for window in (window_first, window_rest):
             nc.vector.memset(window[:], 0.0)
-        nc.gpsimd.dma_start(out=wt_w[:].bitcast(I32), in_=wt_words[0].bitcast(I32))
         nc.gpsimd.dma_start(
             out=wa_w[:].bitcast(I32), in_=wat_words[:, 0].rearrange("e p x -> p e x").bitcast(I32)
         )
@@ -94,6 +93,7 @@ def tile_moe_adb_none_kernel(
         )
         load_planes((nc.sync, nc.scalar), wb_s, wbt_scales[:, 0])
         load_planes((nc.sync,), wa_s, wat_scales[:, 0])
+        nc.sync.dma_start(out=wt_w[:].bitcast(I32), in_=wt_words[0].bitcast(I32))
         load_planes((nc.sync,), wt_s, wt_scales)
 
         slot_w = laid.tile([P, T], U32, name="slot_w", align_bytes=ALIGN, offset=C)

@@ -160,23 +160,25 @@ def tile_moe_adb_none_kernel(
                 in_=dh_by_i[:, 4 * slots.start : 4 * slots.stop],
             )
 
-        def second_product(b0, b1, bank, dx, copy, tokens=None):
+        def second_product(b0, b1, bank, dx, copy):
             slots = slots_of(b0, b1)
             width = slots.stop - slots.start
-            sums = psum.tile([P, T], F32, name="sums_x", tag=bank)
+            sums = psum.tile([P, width], F32, name="sums_x", tag=bank)
             e = b0 * GROUP // C
             nc.tensor.matmul_mx(
                 out=sums[:, :width],
                 lhsT=wa_w[:, e, :].bitcast(FP4X4), lhsT_scale=wa_s[:, e, :],
                 rhs=dh_w[:, slots].bitcast(FP8X4), rhs_scale=dh_s[:, slots], start=True, stop=True,
             )
-            if tokens is not None:
-                nc.tensor.matmul_mx(
-                    out=sums[:, C:], lhsT=wt_w[:].bitcast(FP4X4), lhsT_scale=wt_s[:, 0, :],
-                    rhs=dy_w[:, tokens].bitcast(FP8X4), rhs_scale=dy_s[:, tokens], start=True, stop=True,
-                )
             copy(out=dx, in_=sums[:, :width])
-            return sums[:, C:]
+
+        def frozen_layer(bank, tokens):
+            sums = psum.tile([P, C], F32, name="sums_base", tag=bank)
+            nc.tensor.matmul_mx(
+                out=sums[:], lhsT=wt_w[:].bitcast(FP4X4), lhsT_scale=wt_s[:, 0, :],
+                rhs=dy_w[:, tokens].bitcast(FP8X4), rhs_scale=dy_s[:, tokens], start=True, stop=True,
+            )
+            return sums[:]
 
         for e in range(E):
             gather_scales(e)
@@ -198,10 +200,9 @@ def tile_moe_adb_none_kernel(
         nc.vector.tensor_copy(window_rest[:].indirect(offsets_of(slots_of(0, 1))), dx[0][:])
         nc.scalar.activation(out=window_first[:].indirect(offsets_of(slots_of(1, 2))), in_=dx[1][:], func=COPY)
         stores = ((nc.sync, slice(0, C)), (nc.scalar, slice(C, T)))
-        base = [
-            second_product(2, 3, "G", dx[2][:], nc.scalar.copy, stores[0][1]),
-            second_product(3, 4, "H", dx[3][:], nc.vector.tensor_copy, stores[1][1]),
-        ]
+        second_product(2, 3, "G", dx[2][:], nc.scalar.copy)
+        second_product(3, 4, "H", dx[3][:], nc.vector.tensor_copy)
+        base = [frozen_layer("H", stores[0][1]), frozen_layer("G", stores[1][1])]
         nc.scalar.activation(out=window_first[:].indirect(offsets_of(slots_of(2, 3))), in_=dx[2][:], func=COPY)
         nc.vector.tensor_copy(window_rest[:].indirect(offsets_of(slots_of(3, 4))), dx[3][:])
         partial = keep.tile([P, T], F32, name="partial", align_bytes=ALIGN)

@@ -1,7 +1,6 @@
 from contextlib import ExitStack
 
 import concourse.mybir as mybir
-from concourse.masks import make_identity
 
 K, T, E, C, H, N = 128, 512, 2, 256, 512, 512
 FLOPS = 2 * (N * K * T + N * H * T + H * K * T)
@@ -57,6 +56,7 @@ def tile_moe_adb_none_kernel(
     with ExitStack() as ctx:
         keep = ctx.enter_context(tc.tile_pool(name="keep", bufs=1))
         laid = ctx.enter_context(tc.tile_pool(name="laid", bufs=1))
+        early = ctx.enter_context(tc.tile_pool(name="early", bufs=1))
         psum = ctx.enter_context(tc.psum_pool(name="psum", bufs=1))
 
         offsets = keep.tile([P, T // PER_COLUMN], U16, name="offsets")
@@ -64,7 +64,7 @@ def tile_moe_adb_none_kernel(
         dy_s = keep.tile([P, T], U8, name="dy_s", align_bytes=ALIGN)
         wb_w = keep.tile([P, E, 2 * H], U8, name="wb_w", align_bytes=ALIGN)
         wb_s = keep.tile([P, E, H], U8, name="wb_s", align_bytes=ALIGN)
-        wa_w = keep.tile([P, E, 2 * K], U8, name="wa_w", align_bytes=ALIGN)
+        cleared = early.tile([P, P], F32, name="cleared", align_bytes=ALIGN, offset=0)
         wa_s = keep.tile([P, E, K], U8, name="wa_s", align_bytes=ALIGN)
         wt_w = keep.tile([P, 2 * K], U8, name="wt_w", align_bytes=ALIGN)
         wt_s = keep.tile([P, 1, K], U8, name="wt_s", align_bytes=ALIGN)
@@ -78,10 +78,15 @@ def tile_moe_adb_none_kernel(
         window_rest = keep.tile([P, T], F32, name="window_rest", align_bytes=ALIGN)
         for window in (window_first, window_rest):
             nc.vector.memset(window[:], 0.0)
+        nc.gpsimd.memset(cleared[:], 0.0)
+        nc.gpsimd.affine_select(
+            out=identity[:], in_=cleared[:], compare_op=mybir.AluOpType.not_equal, fill=1.0, base=0,
+            pattern=[[-1, P]], channel_multiplier=1,
+        )
+        wa_w = early.tile([P, E, 2 * K], U8, name="wa_w", align_bytes=ALIGN, offset=0)
         nc.gpsimd.dma_start(
             out=wa_w[:].bitcast(I32), in_=wat_words[:, 0].rearrange("e p x -> p e x").bitcast(I32)
         )
-        make_identity(nc, identity[:])
 
         nc.sync.dma_start(offsets[:], offs)
         load_plane_filled((nc.scalar, nc.sync), dy_s, dy_scales[0])
@@ -201,8 +206,8 @@ def tile_moe_adb_none_kernel(
         nc.scalar.activation(out=window_first[:].indirect(offsets_of(slots_of(1, 2))), in_=dx[1][:], func=COPY)
         stores = ((nc.sync, slice(0, C)), (nc.scalar, slice(C, T)))
         second_product(2, 3, "G", dx[2][:], nc.scalar.copy)
-        second_product(3, 4, "H", dx[3][:], nc.vector.tensor_copy)
-        base = [frozen_layer("H", stores[0][1]), frozen_layer("G", stores[1][1])]
+        second_product(3, 4, "E", dx[3][:], nc.vector.tensor_copy)
+        base = [frozen_layer("E", stores[0][1]), frozen_layer("G", stores[1][1])]
         nc.scalar.activation(out=window_first[:].indirect(offsets_of(slots_of(2, 3))), in_=dx[2][:], func=COPY)
         nc.vector.tensor_copy(window_rest[:].indirect(offsets_of(slots_of(3, 4))), dx[3][:])
         partial = keep.tile([P, T], F32, name="partial", align_bytes=ALIGN)

@@ -24,7 +24,7 @@ PER_COLUMN = 16
 QUADRANTS = 4
 BLOCK = 32
 ALIGN = 64
-FIRST_STORE = 320
+FIRST_SCATTER = 96
 
 
 def load_plane_filled(queues, plane, rows):
@@ -199,17 +199,16 @@ def tile_moe_adb_none_kernel(
         quantise(2, 3)
         turn(3, "D", nc.scalar.copy)
         quantise(3, 4)
-        dx = [keep.tile([P, GROUP], F32, name="dx%d" % b, align_bytes=ALIGN) for b in range(GROUPS)]
-        second_product(0, 1, "E", dx[0][:], nc.scalar.copy)
-        second_product(1, 2, "F", dx[1][:], nc.scalar.copy)
-        nc.vector.tensor_copy(window_rest[:].indirect(offsets_of(slots_of(0, 1))), dx[0][:])
-        nc.scalar.activation(out=window_first[:].indirect(offsets_of(slots_of(1, 2))), in_=dx[1][:], func=COPY)
+        dx = keep.tile([P, T], F32, name="dx", align_bytes=ALIGN)
+        for b, bank in enumerate("EFG"):
+            second_product(b, b + 1, bank, dx[:, slots_of(b, b + 1)], nc.scalar.copy)
+        second_product(3, 4, "E", dx[:, slots_of(3, 4)], nc.vector.tensor_copy)
         stores = ((nc.sync, slice(0, C)), (nc.scalar, slice(C, T)))
-        second_product(2, 3, "G", dx[2][:], nc.scalar.copy)
-        second_product(3, 4, "E", dx[3][:], nc.vector.tensor_copy)
-        base = [frozen_layer("E", stores[0][1]), frozen_layer("G", stores[1][1])]
-        nc.scalar.activation(out=window_first[:].indirect(offsets_of(slots_of(2, 3))), in_=dx[2][:], func=COPY)
-        nc.vector.tensor_copy(window_rest[:].indirect(offsets_of(slots_of(3, 4))), dx[3][:])
+        base = [frozen_layer("F", stores[0][1]), frozen_layer("G", stores[1][1])]
+        middle = slice(FIRST_SCATTER, T - GROUP)
+        for slots in (slice(0, middle.start), slice(middle.stop, T)):
+            nc.vector.tensor_copy(window_rest[:].indirect(offsets_of(slots)), dx[:, slots])
+        nc.scalar.activation(out=window_first[:].indirect(offsets_of(middle)), in_=dx[:, middle], func=COPY)
         partial = keep.tile([P, T], F32, name="partial", align_bytes=ALIGN)
         for half, (queue, cols) in enumerate(stores):
             nc.vector.tensor_tensor(out=partial[:, cols], in0=base[half], in1=window_rest[:, cols], op=ADD)

@@ -83,10 +83,7 @@ def tile_moe_adb_none_kernel(
             out=identity[:], in_=cleared[:], compare_op=mybir.AluOpType.not_equal, fill=1.0, base=0,
             pattern=[[-1, P]], channel_multiplier=1,
         )
-        wa_w = early.tile([P, E, 2 * K], U8, name="wa_w", align_bytes=ALIGN, offset=0)
-        nc.gpsimd.dma_start(
-            out=wa_w[:].bitcast(I32), in_=wat_words[:, 0].rearrange("e p x -> p e x").bitcast(I32)
-        )
+        wa_w = keep.tile([P, E, 2 * K], U8, name="wa_w", align_bytes=ALIGN)
 
         nc.sync.dma_start(offsets[:], offs)
         load_plane_filled((nc.scalar, nc.sync), dy_s, dy_scales[0])
@@ -98,6 +95,7 @@ def tile_moe_adb_none_kernel(
         )
         load_planes((nc.sync, nc.scalar), wb_s, wbt_scales[:, 0])
         load_planes((nc.sync,), wa_s, wat_scales[:, 0])
+        nc.sync.dma_start(out=wa_w[:].bitcast(I32), in_=wat_words[:, 0].rearrange("e p x -> p e x").bitcast(I32))
         nc.sync.dma_start(out=wt_w[:].bitcast(I32), in_=wt_words[0].bitcast(I32))
         load_planes((nc.sync,), wt_s, wt_scales)
 

@@ -201,7 +201,7 @@ def tile_moe_adb_none_kernel(
         for b, bank in enumerate("EFG"):
             second_product(b, b + 1, bank, dx[:, slots_of(b, b + 1)], nc.scalar.copy)
         second_product(3, 4, "E", dx[:, slots_of(3, 4)], nc.vector.tensor_copy)
-        stores = ((nc.sync, slice(0, C)), (nc.scalar, slice(C, T)))
+        stores = ((nc.scalar, slice(0, C)), (nc.scalar, slice(C, T)))
         base = [frozen_layer("F", stores[0][1]), frozen_layer("G", stores[1][1])]
         middle = slice(FIRST_SCATTER, T - GROUP)
         for slots in (slice(0, middle.start), slice(middle.stop, T)):

@@ -24,7 +24,7 @@ PER_COLUMN = 16
 QUADRANTS = 4
 BLOCK = 32
 ALIGN = 64
-FIRST_SCATTER = 96
+FIRST_SCATTER = 64
 
 
 def load_plane_filled(queues, plane, rows):

@@ -183,6 +183,11 @@ def tile_moe_adb_none_kernel(
             )
             return sums[:]
 
+        unread = psum.tile([P, C], F32, name="unread", tag="H")
+        nc.tensor.matmul_mx(
+            out=unread[:], lhsT=wb_w[:, 0, : 2 * P].bitcast(FP4X4), lhsT_scale=dy_s[:, :P],
+            rhs=dy_w[:, :C].bitcast(FP8X4), rhs_scale=dy_s[:, :C], start=True, stop=True,
+        )
         for e in range(E):
             gather_scales(e)
             for b in range(e * C // GROUP, (e + 1) * C // GROUP):

from contextlib import ExitStack

import concourse.mybir as mybir

K, T, E, C, H, N = 128, 512, 2, 256, 512, 512
FLOPS = 2 * (N * K * T + N * H * T + H * K * T)

F32 = mybir.dt.float32
BF16 = mybir.dt.bfloat16
I32 = mybir.dt.int32
U32 = mybir.dt.uint32
U16 = mybir.dt.uint16
U8 = mybir.dt.uint8
FP8X4 = mybir.dt.float8_e4m3fn_x4
FP4X4 = mybir.dt.float4_e2m1fn_x4
COPY = mybir.ActivationFunctionType.Copy
ADD = mybir.AluOpType.add
MULT = mybir.AluOpType.mult

P = 128
GROUP = 128
GROUPS = T // GROUP
PER_COLUMN = 16
QUADRANTS = 4
BLOCK = 32
ALIGN = 64
FIRST_SCATTER = 64


def load_plane_filled(queues, plane, rows):
    words = rows.bitcast(I32)
    width = words.shape[1]
    for q in range(QUADRANTS):
        repeated = words[4 * q : 4 * q + 4, :].unsqueeze(0).broadcast_to([8, 4, width])
        queues[q % len(queues)].dma_start(out=plane[32 * q : 32 * q + 32, :].bitcast(I32), in_=repeated)


def load_planes(queues, planes, rows):
    words = rows.bitcast(I32).rearrange("e c x -> c e x")
    for q in range(QUADRANTS):
        queues[q % len(queues)].dma_start(
            out=planes[32 * q : 32 * q + 4, :, :].bitcast(I32), in_=words[4 * q : 4 * q + 4, :, :]
        )


def gate_pieces(gate):
    pitch = 2 * T + BLOCK // 4
    spans = gate.rearrange("r c -> (r c)")[: 16 * pitch].rearrange("(u x) -> u x", x=pitch)[:, : 2 * T]
    return spans.rearrange("u (v a) -> u v a", a=GROUP)[:, :, :BLOCK]


def tile_moe_adb_none_kernel(
    tc, dy_words, dy_scales, wt_words, wt_scales, wbt_words, wbt_scales, wat_words, wat_scales, gate, offs, out
):
    nc = tc.nc
    with ExitStack() as ctx:
        keep = ctx.enter_context(tc.tile_pool(name="keep", bufs=1))
        laid = ctx.enter_context(tc.tile_pool(name="laid", bufs=1))
        early = ctx.enter_context(tc.tile_pool(name="early", bufs=1))
        psum = ctx.enter_context(tc.psum_pool(name="psum", bufs=1))

        offsets = keep.tile([P, T // PER_COLUMN], U16, name="offsets")
        dy_w = keep.tile([P, T], U32, name="dy_w", align_bytes=ALIGN)
        dy_s = keep.tile([P, T], U8, name="dy_s", align_bytes=ALIGN)
        wb_w = keep.tile([P, E, 2 * H], U8, name="wb_w", align_bytes=ALIGN)
        wb_s = keep.tile([P, E, H], U8, name="wb_s", align_bytes=ALIGN)
        cleared = early.tile([P, P], F32, name="cleared", align_bytes=ALIGN, offset=0)
        wa_s = keep.tile([P, E, K], U8, name="wa_s", align_bytes=ALIGN)
        wt_w = keep.tile([P, 2 * K], U8, name="wt_w", align_bytes=ALIGN)
        wt_s = keep.tile([P, 1, K], U8, name="wt_s", align_bytes=ALIGN)
        gate_runs = laid.tile([P, BLOCK], F32, name="gate_runs", align_bytes=ALIGN, offset=C - ALIGN)
        gates = keep.tile([P, BLOCK], F32, name="gates", align_bytes=ALIGN)
        identity = keep.tile([P, P], F32, name="identity")

        for planes in (wb_s, wa_s, wt_s):
            nc.vector.memset(planes[:].bitcast(I32), 0)
        window_first = keep.tile([P, T], F32, name="window_first", align_bytes=ALIGN)
        window_rest = keep.tile([P, T], F32, name="window_rest", align_bytes=ALIGN)
        for window in (window_first, window_rest):
            nc.vector.memset(window[:], 0.0)
        nc.gpsimd.memset(cleared[:], 0.0)
        nc.gpsimd.affine_select(
            out=identity[:], in_=cleared[:], compare_op=mybir.AluOpType.not_equal, fill=1.0, base=0,
            pattern=[[-1, P]], channel_multiplier=1,
        )
        wa_w = keep.tile([P, E, 2 * K], U8, name="wa_w", align_bytes=ALIGN)

        nc.sync.dma_start(offsets[:], offs)
        load_plane_filled((nc.scalar, nc.sync), dy_s, dy_scales[0])
        nc.sync.dma_start(out=gate_runs[:], in_=gate_pieces(gate))
        nc.vector.transpose(gates[:], gate_runs[:])
        nc.scalar.dma_start(out=dy_w[:].bitcast(I32), in_=dy_words[0].rearrange("p t d -> p (t d)").bitcast(I32))
        nc.scalar.dma_start(
            out=wb_w[:].bitcast(I32), in_=wbt_words[:, 0].rearrange("e p x -> p e x").bitcast(I32)
        )
        load_planes((nc.sync, nc.scalar), wb_s, wbt_scales[:, 0])
        load_planes((nc.sync,), wa_s, wat_scales[:, 0])
        nc.sync.dma_start(out=wa_w[:].bitcast(I32), in_=wat_words[:, 0].rearrange("e p x -> p e x").bitcast(I32))
        nc.sync.dma_start(out=wt_w[:].bitcast(I32), in_=wt_words[0].bitcast(I32))
        load_planes((nc.sync,), wt_s, wt_scales)

        slot_w = laid.tile([P, T], U32, name="slot_w", align_bytes=ALIGN, offset=C)
        slot_s = [
            keep.tile([P, C], U8, name="slot_s0", align_bytes=ALIGN),
            laid.tile([P, C], U8, name="slot_s1", align_bytes=ALIGN, offset=0),
        ]
        dh_by_slot = [keep.tile([P, H], BF16, name="dh_by_slot%d" % b, align_bytes=ALIGN) for b in range(GROUPS)]
        dh_by_i = keep.tile([P, 4 * T], BF16, name="dh_by_i", align_bytes=ALIGN)
        dh_w = keep.tile([P, T], U32, name="dh_w", align_bytes=ALIGN)
        dh_s = keep.tile([P, T], U8, name="dh_s", align_bytes=ALIGN)

        def slots_of(b0, b1):
            return slice(b0 * GROUP, b1 * GROUP)

        def offsets_of(slots):
            return offsets[:, slots.start // PER_COLUMN : slots.stop // PER_COLUMN]

        def gather_scales(e):
            nc.vector.tensor_copy(slot_s[e][:], dy_s[:].indirect(offsets_of(slice(e * C, (e + 1) * C))))

        def gather_words(b):
            slots = slots_of(b, b + 1)
            nc.vector.tensor_copy(slot_w[:, slots], dy_w[:].indirect(offsets_of(slots)))

        def round_on_scalar(out, sums, weight):
            nc.scalar.activation(out=out, in_=sums, func=COPY, scale=weight)

        def round_on_vector(out, sums, weight):
            nc.vector.tensor_scalar(out=out, in0=sums, scalar1=weight, scalar2=None, op0=MULT)

        def first_product(b, banks):
            e, s0 = divmod(b * GROUP, C)
            place = dh_by_slot[b][:].rearrange("s (u p v) -> s u p v", u=2, v=2)
            for half, gate_and_round in enumerate((round_on_scalar, round_on_vector)):
                i0, i1 = half * H // 2, (half + 1) * H // 2
                sums = psum.tile([P, H // 2], F32, name="sums_h", tag=banks[half])
                nc.tensor.matmul_mx(
                    out=sums[:],
                    lhsT=slot_w[:, slots_of(b, b + 1)].bitcast(FP8X4), lhsT_scale=slot_s[e][:, s0 : s0 + GROUP],
                    rhs=wb_w[:, e, 2 * i0 : 2 * i1].bitcast(FP4X4), rhs_scale=wb_s[:, e, i0:i1],
                    start=True, stop=True,
                )
                gate_and_round(
                    place[:, :, i0 // 4 : i1 // 4, :],
                    sums[:].rearrange("s (p u v) -> s u p v", u=2, v=2),
                    gates[:, b : b + 1],
                )

        def turn(b, bank, copy):
            pairs = dh_by_slot[b][:].bitcast(F32)
            turned = psum.tile([P, 2, GROUP], F32, name="turned", tag=bank)
            for u in range(2):
                nc.tensor.transpose(turned[:, u, :], pairs[:, u * P : (u + 1) * P], identity[:])
            copy(
                out=dh_by_i[:, 4 * b * GROUP : 4 * (b + 1) * GROUP].bitcast(F32).rearrange("p (s u) -> p s u", u=2),
                in_=turned[:].rearrange("p u s -> p s u"),
            )

        def quantise(b0, b1):
            slots = slots_of(b0, b1)
            nc.vector.quantize_mx(
                out=dh_w[:, slots].bitcast(FP8X4), scales=dh_s[:, slots],
                in_=dh_by_i[:, 4 * slots.start : 4 * slots.stop],
            )

        def second_product(b0, b1, bank, dx, copy):
            slots = slots_of(b0, b1)
            width = slots.stop - slots.start
            sums = psum.tile([P, width], F32, name="sums_x", tag=bank)
            e = b0 * GROUP // C
            nc.tensor.matmul_mx(
                out=sums[:, :width],
                lhsT=wa_w[:, e, :].bitcast(FP4X4), lhsT_scale=wa_s[:, e, :],
                rhs=dh_w[:, slots].bitcast(FP8X4), rhs_scale=dh_s[:, slots], start=True, stop=True,
            )
            copy(out=dx, in_=sums[:, :width])

        def frozen_layer(bank, tokens):
            sums = psum.tile([P, C], F32, name="sums_base", tag=bank)
            nc.tensor.matmul_mx(
                out=sums[:], lhsT=wt_w[:].bitcast(FP4X4), lhsT_scale=wt_s[:, 0, :],
                rhs=dy_w[:, tokens].bitcast(FP8X4), rhs_scale=dy_s[:, tokens], start=True, stop=True,
            )
            return sums[:]

        unread = psum.tile([P, C], F32, name="unread", tag="H")
        nc.tensor.matmul_mx(
            out=unread[:], lhsT=wb_w[:, 0, : 2 * P].bitcast(FP4X4), lhsT_scale=dy_s[:, :P],
            rhs=dy_w[:, :C].bitcast(FP8X4), rhs_scale=dy_s[:, :C], start=True, stop=True,
        )
        for e in range(E):
            gather_scales(e)
            for b in range(e * C // GROUP, (e + 1) * C // GROUP):
                gather_words(b)
        for b, banks in enumerate(("AB", "CD", "EF", "GH")):
            first_product(b, banks)
        turn(0, "A", nc.vector.tensor_copy)
        quantise(0, 1)
        turn(1, "B", nc.scalar.copy)
        quantise(1, 2)
        turn(2, "C", nc.scalar.copy)
        quantise(2, 3)
        turn(3, "D", nc.scalar.copy)
        quantise(3, 4)
        dx = keep.tile([P, T], F32, name="dx", align_bytes=ALIGN)
        for b, bank in enumerate("EFG"):
            second_product(b, b + 1, bank, dx[:, slots_of(b, b + 1)], nc.scalar.copy)
        second_product(3, 4, "E", dx[:, slots_of(3, 4)], nc.vector.tensor_copy)
        stores = ((nc.scalar, slice(0, C)), (nc.scalar, slice(C, T)))
        base = [frozen_layer("F", stores[0][1]), frozen_layer("G", stores[1][1])]
        middle = slice(FIRST_SCATTER, T - GROUP)
        for slots in (slice(0, middle.start), slice(middle.stop, T)):
            nc.vector.tensor_copy(window_rest[:].indirect(offsets_of(slots)), dx[:, slots])
        nc.scalar.activation(out=window_first[:].indirect(offsets_of(middle)), in_=dx[:, middle], func=COPY)
        partial = keep.tile([P, T], F32, name="partial", align_bytes=ALIGN)
        for half, (queue, cols) in enumerate(stores):
            nc.vector.tensor_tensor(out=partial[:, cols], in0=base[half], in1=window_rest[:, cols], op=ADD)
        for queue, cols in stores:
            result = keep.tile([P, cols.stop - cols.start], F32, name="result%d" % cols.start, align_bytes=ALIGN)
            nc.vector.tensor_tensor(out=result[:], in0=partial[:, cols], in1=window_first[:, cols], op=ADD)
            queue.dma_start(out=out[:, cols], in_=result[:])
